import numpy as np, ml_dtypes
CORES = [3,7,11,15,131,135,139,143]
N = 8
BF = ml_dtypes.bfloat16
def gentries(a):
    return np.ascontiguousarray(a.reshape(8, 16, -1).transpose(0, 2, 1)).reshape(8, -1)
def gtable(e):
    e = np.asarray(e); return np.ascontiguousarray(e.reshape(8, -1, 16).transpose(0, 2, 1)).reshape(128, -1).astype(np.int32)
W, LN, RO, BL, LG = 2048, 64, 3, 8, 11
SZ = W // LN
DIST = 1 + (np.arange(LN) // BL) % (N - 1)
ROT = (np.arange(16)[:, None] + np.arange(16)[None, :]) % 16
PAT = 255 * np.array([0, 0, 0, 0, 1, 0, 0, 1, 1, 0, 1, 0, 1, 1, 1, 1])
def parts(rng):
    x = rng.integers(0, 256, (N, 8, 16, W)); L = rng.integers(0, W, (N, 8, LN, 16)); c = rng.integers(0, W, (N, 8, LN))
    s = rng.choice(np.array([1.0, 1.3, 1.6]), (N, 8, LN, 1))
    z = np.minimum(np.maximum(np.rint(127.5 + s * (255 * rng.random((N, 8, LN, 16)) - 127.5)), 0), 255).astype(np.int64)
    return x, L, c, z
def mid(rng, x, z, q):
    a = rng.integers(0, W, 512); b = rng.integers(0, LN, 512)
    zz = np.roll(z[:, :, b, :], 5, axis=3).transpose(0, 1, 3, 2)
    d = np.sort(np.sum(np.abs(x[:, :, :, a] - zz), axis=2), axis=2)
    return np.minimum(np.maximum(np.take_along_axis(d, (q * 512).astype(np.int64)[:, :, None], 2)[:, :, 0], 1275), 2295)
def pack(x, L, c, z, t):
    return {"x": x.reshape(N, 128, W).astype(np.float32).astype(BF), "ls": np.stack([gtable(a) for a in L]), "an": c.astype(np.int32),
            "z": np.ascontiguousarray(z.transpose(0, 1, 3, 2)).reshape(N, 128, LN).astype(np.float32).astype(BF), "th": t.reshape(N, 8, 1).astype(np.int32)}
def setup_inputs(rng):
    x, L, c, z = parts(rng)
    return pack(x, L, c, z, mid(rng, x, z, rng.choice(np.array([0.15, 0.22, 0.3, 0.4]), (N, 8))))
def rough(rng, shape, share):
    e = np.minimum(np.exp2(8.1 * rng.random(shape)).astype(np.int64) - 1, 255)
    return np.where(rng.random(shape) < share, 255 - e, e)
def setup_inputs_spread(rng):
    sh = np.array([0.2, 0.5, 0.8])
    x = rough(rng, (N, 8, 16, W), rng.choice(sh, (N, 8, 1, W))); z = rough(rng, (N, 8, LN, 16), rng.choice(sh, (N, 8, LN, 1)))
    e = np.exp2(LG * rng.random((N, 8, LN, 17))).astype(np.int64) - 1
    e = np.where(rng.random(e.shape) < 0.5, W - 1 - e, e)
    return pack(x, e[..., :16], e[..., 16], z, mid(rng, x, z, 0.05 + 0.9 * rng.random((N, 8))))
def setup_inputs_ends(rng):
    sh = np.array([0.3, 0.5, 0.7])
    x = 255 * (rng.random((N, 8, 16, W)) < rng.choice(sh, (N, 8, 1, W))).astype(np.int64)
    z = 255 * (rng.random((N, 8, LN, 16)) < rng.choice(sh, (N, 8, LN, 1))).astype(np.int64)
    L = (W - 1) * (rng.random((N, 8, LN, 16)) < rng.choice(np.array([0.25, 0.5, 0.75]), (N, 8, LN, 1))).astype(np.int64)
    c = (W - 1) * rng.integers(0, 2, (N, 8, LN))
    t = np.where(rng.random((N, 8)) < 0.5, 1275, 2295); t[:, 2] = 1275; t[:, 5] = 2295
    x[:, 1::2, :, 0] = 255; x[:, 1::2, :, W - 1] = 0
    for l, a, b in ((0, 0, 0), (1, W - 1, 0), (2, 0, 255), (3, W - 1, 255), (LN - 4, 0, 0), (LN - 3, W - 1, 255), (LN - 2, W - 1, 0), (LN - 1, 0, 255)):
        L[:, 1::2, l] = 0; c[:, 1::2, l] = a; z[:, 1::2, l] = b
    return pack(x, L, c, z, t)
def setup_inputs_corners(rng):
    x, L, c, z = parts(rng); t = rng.choice(np.array([1275, 1400, 1600, 1800]), (N, 8))
    cnt = np.minimum(np.array([0, 1, 31, 32, 33, LN - 1, LN, 9]), LN)
    for q in range(N):
        order = np.arange(8) if q == 0 else rng.permutation(8)
        for g in range(8):
            hot = rng.permutation(LN) < cnt[order[g]]
            for l in range(LN):
                m = int(rng.choice(np.array([16, 16, 15, 9, 17]))) if hot[l] else int(rng.choice(np.array([8, 8, 1, 0])))
                col = SZ * l + 8 + int(rng.integers(0, 16)); kk = int(rng.choice(np.array([0, 15, int(rng.integers(0, 16))]))) if m == 16 else 0
                zz = np.full(16, 255) if m == 17 else np.roll(PAT, int(rng.integers(0, 16)))
                x[q, g][:, [col - 6, col + 1, col + 6]] = rng.integers(120, 136, (16, 3))
                x[q, g, :, col] = rng.integers(120, 136, 16) if m == 0 else np.roll(zz, -kk)
                c[q, g, l] = col; z[q, g, l] = zz
                L[q, g, l] = 0 if m in (0, 16, 17) else np.where(rng.permutation(16) < m, 0, 6)
    return pack(x, L, c, z, t)
def setup_inputs_ties(rng):
    x, L, c, z = parts(rng); t = mid(rng, x, z, rng.choice(np.array([0.2, 0.3, 0.4]), (N, 8)))
    t[:, ::2] = rng.integers(1275, 2296, (N, 4)); t[0, 0] = 1275; t[N - 1, 6] = 2295
    s = t[:, ::2, None] + rng.integers(-1, 2, (N, 4, LN)); up = rng.random((N, 4, LN)) < 0.5; m = rng.random((N, 4, LN)) < 0.6
    v = (s // 16)[:, :, None, :] + (np.arange(16)[:, None] < (s % 16)[:, :, None, :])
    v = np.where(up[:, :, None, :], 255 - v, v); col = SZ * np.arange(LN) + rng.integers(0, SZ, (N, 4, LN))
    xe = x[:, ::2]; np.put_along_axis(xe, np.repeat(col[:, :, None, :], 16, axis=2), v, 3)
    L[:, ::2] = np.where(m[..., None], 0, L[:, ::2]); c[:, ::2] = np.where(m, col, c[:, ::2]); z[:, ::2] = np.where(m[..., None], 255 * up[..., None], z[:, ::2])
    L[:, 1] = L[:, 1, :1].copy(); c[:, 1] = c[:, 1, :1].copy(); z[:, 1] = z[:, 1][:, np.arange(LN) % 2]
    L[:, 3] = 0; c[:, 3] = W - 1; c[1::2, 3, LN - 1] = 0
    L[:, 5] = rng.choice(np.array([0, 3, W // 2, W - 1]), (N, LN, 16))
    x[:, 7, :, 1::2] = x[:, 7, :, ::2].copy(); L[:, 7, 1::2] = L[:, 7, ::2].copy(); c[:, 7, 1::2] = c[:, 7, ::2].copy()
    return pack(x, L, c, z, t)
def check_inputs(d):
    bad = []
    for k, lo, hi in (("x", 0, 255), ("ls", 0, W - 1), ("an", 0, W - 1), ("z", 0, 255), ("th", 1275, 2295)):
        v = np.asarray(d[k]).astype(np.float64)
        if not (np.min(v) >= lo and np.max(v) <= hi): bad.append("range of " + k)
        elif np.any(v != np.floor(v)): bad.append("whole numbers in " + k)
    return bad
def reference(x, ls, an, z, th):
    X = x.astype(np.float32).astype(np.int64).reshape(N, 8, 16, W)
    L = np.stack([gentries(a) for a in ls]).astype(np.int64).reshape(N, 8, LN, 16)
    c = an.astype(np.int64)
    Z = z.astype(np.float32).astype(np.int64).reshape(N, 8, 16, LN).transpose(0, 1, 3, 2)
    t = th.astype(np.int64).reshape(N, 8); A = np.zeros((N, 8), np.int64)
    src = ((np.arange(N)[:, None] - DIST[None, :]) % N)[:, None, :]; gg = np.arange(8)[None, :, None]; sl = np.arange(LN)[None, None, :]
    k16 = np.arange(16)
    for rnd in range(RO):
        La = L[:, :, :, ROT]; Li = L[:, :, :, None, :]
        E = (((La * Li) >> 5) + La - Li + c[:, :, :, None, None]) & (W - 1)
        ix = E.reshape(N, 8, LN * 256); D = np.zeros(E.shape, np.int64)
        for f in range(16):
            D = D + np.abs(np.take_along_axis(X[:, :, f], ix, 2).reshape(E.shape) - Z[:, :, :, (f + k16) % 16][..., None])
        C = np.sum(D < (t + (A & 31))[:, :, None, None, None], axis=4)
        kt = np.argmax(C, axis=3); kb = np.argmin(C, axis=3)
        win = np.take_along_axis(E, kt[..., None, None], 3)[:, :, :, 0]
        v = np.take_along_axis(np.take_along_axis(E, kb[..., None, None], 3)[:, :, :, 0], kt[..., None], 3)
        M = np.max(np.take_along_axis(X, np.repeat(win.reshape(N, 8, 1, LN * 16), 16, axis=2), 3).reshape(N, 8, 16, LN, 16), axis=4).transpose(0, 1, 3, 2)
        Y = (M + Z) >> 1
        u = np.sum(Y * (2 * k16 + 1), axis=3) & (W - 1)
        A = np.sum(np.max(C, axis=3) >= 9, axis=2)
        place = SZ * np.arange(LN) + (u & (SZ - 1))
        np.put_along_axis(X, np.repeat(place[:, :, None, :], 16, axis=2), Y.transpose(0, 1, 3, 2), 3)
        c = (((u * u) >> 5) + 37 * u + A[:, :, None]) & (W - 1)
        Z = np.abs(Z - M)
        L = np.where(np.roll(k16 == kb[..., None], 1, axis=0), np.roll(v, 1, axis=0), win)
        L = L[src, gg, sl]; c = c[src, gg, sl]; Z = Z[src, gg, sl]
    return {"yx": X.reshape(N, 128, W).astype(np.float32).astype(BF), "yl": np.stack([gtable(a) for a in L]).astype(np.float32), "ya": c.astype(np.float32),
            "yz": np.ascontiguousarray(Z.transpose(0, 1, 3, 2)).reshape(N, 128, LN).astype(np.float32).astype(BF)}

@@ -1,0 +1,500 @@
+from concourse.bass import DstId, RemoteDMATransfer
+from concourse.mybir import AluOpType as OP, AxisListType, ActivationFunctionType as AF
+
+NR, RO, W = 8, 3, 2048
+HALF = (32, 0)
+DISTS = ((5, 6, 7, 1, 2), (1, 2, 3, 4, 5))
+KINDS = ["AADADDAADDDADAAD", "DDAADDAADDABDDBA"] + ["DDAADDAADDAAADAD", "DBDDBDAADDBBDABA"] * 2
+OPT = {"names": 5, "late": 10, "look": 90.0, "rmv": 6, "split": 256, "pieces": (4, 4, 8), "gap": 30.0, "start": (4, 4, 8), "write": 3000.0}
+ORDER = {}
+
+F, B, H, I, U = "float32", "bfloat16", "float16", "int32", "uint16"
+SCRATCH = {
+    "X0": ("sbuf", [128, W], B), "jb": ("sbuf", [128, 4], F), "base": ("sbuf", [128, 4], F),
+    "lsi": ("sbuf", [128, 64], I), "zin": ("sbuf", [128, 64], B), "ani": ("sbuf", [128, 72], I), "anh": ("sbuf", [128, 72], H),
+    "jc": ("sbuf", [128, 144], B), "jg": ("sbuf", [128, 128], B), "jm": ("sbuf", [128, 64], F), "ja": ("sbuf", [128, 2], F),
+    "jh": ("sbuf", [128, 512], B), "jk": ("sbuf", [128, 32], F), "jl": ("sbuf", [128, 32], F), "jp": ("sbuf", [128, 20], I),
+    "pq": ("sbuf", [128, 20], I), "cols": ("sbuf", [128, 32], F), "i16": ("sbuf", [128, 16], F),
+    "Pm": ("sbuf", [128, 2048], B), "Rm": ("sbuf", [128, 2048], B),
+    "BO": ("sbuf", [128, 128], B), "Wt": ("sbuf", [128, 128], B), "In": ("sbuf", [128, 128], B),
+    "W1": ("sbuf", [128, 144], B), "W2": ("sbuf", [128, 144], B), "Wn": ("sbuf", [128, 144], B), "W5": ("sbuf", [128, 144], B),
+    "one": ("sbuf", [128, 512], B), "seg": ("sbuf", [128, 512], B), "rst": ("sbuf", [128, 64], F),
+    "gt": ("sbuf", [128, 64], F), "pick": ("sbuf", [128, 64], F), "al": ("sbuf", [128, 2], U),
+    "hot": ("sbuf", [128, 512], B), "ktab": ("sbuf", [128, 32], F), "sl": ("sbuf", [128, 32], U),
+    "SB": ("sbuf", [128, 240, 5], H), "RB": ("sbuf", [128, 240, 5], H), "RA": ("sbuf", [128, 24], F),
+    "Tm": ("sbuf", [128, 4], F), "Tb": ("sbuf", [128, 4], F), "Ac": ("sbuf", [128, 12], F),
+    "Ai": ("sbuf", [128, 8], I),
+    "L16": ("sbuf", [128, 64], H), "Lp": ("sbuf", [128, 64], F), "K": ("sbuf", [128, 64], F), "Kc": ("sbuf", [128, 32], F),
+    "ta": ("sbuf", [128, 64], F), "tb": ("sbuf", [128, 64], F),
+    "La": ("sbuf", [128, 1024], F), "Zs": ("sbuf", [128, 2048], B), "pr": ("sbuf", [128, 1024], F),
+    "Ni": ("sbuf", [128, 1024], I), "Ei": ("sbuf", [128, 1024], I), "O": ("sbuf", [128, 1024], U),
+    "d": ("sbuf", [128, 16384], B), "r": ("sbuf", [128, 16384], B),
+    "ind0": ("sbuf", [128, 2, 16, 16], B), "ind1": ("sbuf", [128, 2, 16, 16], B),
+    "key": ("sbuf", [128, 64], F), "ksc": ("sbuf", [128, 2, 64], F), "ki": ("sbuf", [128, 8], I), "ok": ("sbuf", [128, 4], U),
+    "ia": ("sbuf", [128, 4], B), "pw": ("sbuf", [128, 32], F), "nw": ("sbuf", [128, 32], I), "wi": ("sbuf", [128, 32], I),
+    "ow": ("sbuf", [128, 32], U), "wh": ("sbuf", [128, 32], F), "Gb": ("sbuf", [128, 512], B), "Mx": ("sbuf", [128, 512], B),
+    "sm": ("sbuf", [128, 32], F), "Yi": ("sbuf", [128, 32], I), "Y": ("sbuf", [128, 64], B), "ui": ("sbuf", [128, 32], I),
+    "um": ("sbuf", [128, 32], I), "ut": ("sbuf", [128, 32], F), "up": ("sbuf", [128, 32], I), "uc": ("sbuf", [128, 32], I),
+    "us": ("sbuf", [128, 64], F), "u31": ("sbuf", [128, 12], I), "pl": ("sbuf", [128, 4], U),
+    "oL": ("sbuf", [128, 64], F), "oz": ("sbuf", [128, 64], B), "on": ("sbuf", [128, 64], F), "oi": ("sbuf", [128, 64], I),
+    "oj": ("sbuf", [128, 64], I), "oa": ("sbuf", [128, 64], F),
+    "pD0": ("psum", [128, 512], F), "pD1": ("psum", [128, 512], F), "pS0": ("psum", [128, 512], F), "pS1": ("psum", [128, 512], F),
+    "pLa": ("psum", [128, 512], F), "pLi": ("psum", [128, 512], F), "pZ": ("psum", [128, 512], F), "pM": ("psum", [128, 512], F),
+}
+NDMA = 12
+SEMAPHORES = ["V", "S", "P", "G", "sent"] + ["dma%d" % k for k in range(NDMA)] + ["arr%d" % k for k in range(3 * RO)]
+
+CYC, PEC, GAT, LAT = 1.04, 0.52, 1.56, 70.0
+NOW = 1e9
+
+
+def runs(kinds):
+    out, i = [], 0
+    while i < 16:
+        n = 2 if i % 4 < 3 and kinds[i + 1] == kinds[i] else 1
+        out.append((i, n)); i += n
+    return out
+
+
+def calls_for(src, dsts, topo, same, apart):
+    near = [j for j, c in enumerate(dsts) if c in topo.cores_of(src)]
+    far = [j for j in range(len(dsts)) if j not in near]
+    out = topo.engines(src, dsts[far[0]])
+    call = [([j], [e for e in topo.engines(src, dsts[j]) if e not in out]) for j in near]
+    if same:
+        return [call + [(far, out)]]
+    ahead = [[([far.pop()], out)]] if apart else []
+    n = len(out) // 4
+    call += [([j], out[n * t:n * t + n] if t + 1 < len(far) else out[n * t:]) for t, j in enumerate(far)]
+    return ahead + [call]
+
+
+def rank_program(g, core, T, topo):
+    rank = T.rank_of(core)
+    if rank is None:
+        return
+    V, S, P = g.vector, g.scalar, g.tensor
+    queue = {"V": V, "S": S, "P": P, "G": g, "Y": g.sync}
+    ops, reg, ndma, sent, pri = [], {}, [0], [0], [NOW]
+
+    def add(eng, fn, cost, rd=(), wr=(), bank=(), kind="c", lat=0.0, after=(), sem=None):
+        o = {"n": len(ops), "eng": eng, "fn": fn, "cost": cost, "kind": kind, "lat": lat, "dep": set(after), "sem": sem, "grp": None,
+             "pri": pri[0]}
+        acc = [(x, "r") for x in rd] + [(x, None) for x in wr] + list(bank)
+        for x, tag in acc:
+            cur, prev = reg.get(x, ((None, []), []))
+            if tag is not None and cur[0] == tag:
+                o["dep"].update(prev); cur[1].append(o["n"])
+            else:
+                o["dep"].update(cur[1]); reg[x] = ((tag, [o["n"]]), cur[1])
+        o["dep"].discard(o["n"])
+        ops.append(o)
+        return o["n"]
+
+    def at(chunk):
+        pri[0] = NOW if chunk is None else -1e6 * chunk
+
+    def vc(n, f=1.0):
+        return 20 + max(64.0, n * f) * CYC
+
+    def gc_(n, base):
+        return base + n * GAT * CYC
+
+    def ts(out, in0, s1, s2, op0, op1, rd, wr, n=32, f=1.0, bank=()):
+        if op1 is None:
+            fn = lambda: V.tensor_scalar(out, in0, s1, None, op0)
+        else:
+            fn = lambda: V.tensor_scalar(out, in0, s1, s2, op0, op1)
+        return add("V", fn, vc(n, f), rd, wr, [(b, "V") for b in bank])
+
+    def tt(out, a, b, op, rd, wr, n=32, bank=(), gat=False):
+        c = gc_(n, 50) if gat else vc(n, 1.0 if bank else 2.0)
+        return add("V", lambda: V.tensor_tensor(out, a, b, op), c, rd, wr, [(x, "V") for x in bank])
+
+    def cp(out, a, rd, wr, n=32, bank=(), c=None):
+        return add("V", lambda: V.tensor_copy(out, a), c or vc(n), rd, wr, [(x, "V") for x in bank])
+
+    def scan(out, a, b, op0, op1, rd, wr, n, bank=()):
+        return add("V", lambda: V.tensor_tensor_scan(out, a, b, 0.0, op0, op1), vc(n), rd, wr, [(x, "V") for x in bank])
+
+    def fill(out, v, wr, n):
+        return add("V", lambda: V.memset(out, v), vc(n), (), wr)
+
+    def act(out, a, func, rd, wr, n, bank=(), gat=False, **kw):
+        return add("S", lambda: S.activation(out, a, func, **kw), gc_(n, 65) if gat else vc(n), rd, wr, [(x, "S") for x in bank])
+
+    def mm(out, lhsT, rhs, bank, tag, rd, n, flags=None):
+        k = add("P", None, max(64, n) * PEC, rd, (), [(bank, tag)])
+        ops[k]["mm"] = (out, lhsT, rhs, flags); ops[k]["grp"] = (bank, tag)
+        return k
+
+    def dma(eng, out, a, rd, wr, lat, cost=60.0, **kw):
+        s = "dma%d" % ndma[0]; ndma[0] += 1
+        return add(eng, lambda: queue[eng].dma_start(out, a, **kw), cost, rd, wr, kind="d", lat=lat, sem=(s, 16))
+
+    def iota(out, pat, base, cm, wr, n, small=True):
+        if small:
+            fn = lambda: g.iota(out, pat, base, cm, allow_small_or_imprecise_dtypes=True)
+        else:
+            fn = lambda: g.iota(out, pat, base, cm)
+        return add("G", fn, 130 + 2 * n * CYC, (), wr)
+
+    def message(no, dists, src_of, dst_of, same, rd, wr, ahead=None):
+        arr = "arr%d" % no
+        dsts = [T.cores[(rank + x) % NR] for x in dists]
+        made = []
+        calls = calls_for(core, dsts, topo, same, ahead is not None)
+        for call in calls:
+            tr = []
+            for js, es in call:
+                ids = [topo.addr(dsts[j], core) for j in js]
+                tr.append(RemoteDMATransfer(dst_ids=[DstId(rid=a, pnc=b) for a, b in ids], dma_engine_mask=sum(1 << e for e in es),
+                                            remote_sem=T.sem[arr], srcs=[src_of(js[0])], dsts=[dst_of(j) for j in js]))
+                sent[0] += len(es)
+            made.append(add("G", lambda tr=tr: g.remote_dma_fused(tr, local_sem=T.sem.sent), 500.0,
+                            rd if call is calls[-1] else ahead, (), kind="s"))
+        total = 0
+        for j, x in enumerate(dists):
+            s = (rank - x) % NR
+            for call in calls_for(T.cores[s], [T.cores[(s + y) % NR] for y in dists], topo, same, ahead is not None):
+                total += sum(len(es) for js, es in call if j in js)
+        add(None, None, 0.0, (), wr, kind="a", lat=4000.0 if same else 4600.0, after=made, sem=(arr, total))
+
+    fill(T.ani[:], 0, ["ani", "thi"], 72)
+    dma("Y", T.lsi[:], T.ls[:], (), ["lsi"], 2000)
+    dma("S", T.zin[:], T.z[:], (), ["zin"], 2000)
+    dma("Y", T.ani[0:128:16, 0:64], T.an[:], (), ["ani"], 2000)
+    dma("S", T.ani[0:128:16, 64:65], T.th[:], (), ["thi"], 2000)
+    dma("Y", T.X0[:], T.x[:], (), ["X"], 4500)
+
+    iota(T.jp[:, 0:17], [[-1, 17]], 16, 1, ["jp"], 17, False)
+    iota(T.jc[:], [[1, 144]], 0, 0, ["jc"], 144)
+    iota(T.jg[:], [[16, 8], [0, 16]], 0, 0, ["jg"], 128)
+    iota(T.jl[:], [[0, 16], [16, 2]], 0, 0, ["jl"], 32)
+    fill(T.one[:], 1.0, ["one"], 256)
+    fill(T.cols[:, 6:7], -32.0, ["c6"], 1)
+    ts(T.pq[:, 0:17], T.jp[:, 0:17], 15, None, OP.bitwise_and, None, ["jp"], ["pq"])
+    cp(T.i16[:], T.pq[:, 0:16], ["pq"], ["i16a"])
+    q = T.i16[:, 0:1]
+    ts(T.cols[:, 1:2], T.jp[:, 16:17], q, None, OP.subtract, None, ["jp", "i16a"], ["c1"])
+    ts(T.cols[:, 16:32], T.i16[:], 0.0, None, OP.is_equal, None, ["i16a"], ["c16"])
+    ts(T.BO[:], T.jg[:], T.cols[:, 1:2], None, OP.is_equal, None, ["jg", "c1"], ["BO"])
+    ts(T.ta[:, 0:16], T.i16[:], T.cols[:, 1:2], None, OP.add, None, ["i16a", "c1"], ["ta0"])
+    rot = [T.Pm[:, 128 * i:128 * i + 128] for i in range(16)]
+    row = [T.Rm[:, 128 * i:128 * i + 128] for i in range(16)]
+    for i in range(16):
+        ts(rot[i], T.jc[:, 0:128], T.ta[:, i:i + 1], None, OP.is_equal, None, ["jc", "ta0"], ["Pm%d" % i])
+    for i in range(16):
+        if i >= OPT["rmv"]:
+            act(row[i], T.BO[:], AF.Identity, ["BO", "c16"], ["Rm%d" % i], 128, scale=T.cols[:, 16 + i:17 + i])
+        else:
+            ts(row[i], T.BO[:], T.cols[:, 16 + i:17 + i], None, OP.mult, None, ["BO", "c16"], ["Rm%d" % i])
+    ts(T.sl[:], T.jl[:], q, None, OP.add, None, ["jl", "i16a"], ["sl"])
+    ts(T.anh[:, 0:65], T.ani[:, 0:65], -1024.0, None, OP.add, None, ["ani", "thi"], ["anh"])
+    mm(T.pM[:, 0:65], row[0], T.anh[:, 0:65], "pM", "an", ["Rm0", "anh"], 65, (True, True))
+    ts(T.K[:], T.pM[:, 0:64], 32.0, 33792.0, OP.mult, OP.add, [], ["K0", "K1"], 64, bank=["pM"])
+    cp(T.L16[:], T.lsi[:], ["lsi"], ["L0", "L1"])
+    at(0)
+    act(T.In[:], rot[0], AF.Identity, ["Pm0"], ["In"], 128, scale=-1.0)
+    ts(T.W1[:], T.jc[:], -15.0, T.cols[:, 1:2], OP.add, OP.is_equal, ["jc", "c1"], ["W1"])
+    act(T.W2[:], T.W1[:], AF.Identity, ["W1"], ["W2"], 144, scale=2.0)
+    act(T.Wn[:], T.W1[:], AF.Identity, ["W1"], ["Wn"], 144, scale=-1.0)
+    at(OPT["late"])
+    iota(T.jk[:], [[16, 2], [32, 16]], 8192, 0, ["jk"], 32)
+    iota(T.jm[:], [[0, 4], [1, 16]], 0, 0, ["jm"], 64)
+    iota(T.jb[:], [[512, 4]], 0, 0, ["jb"], 4)
+    iota(T.ja[:], [[2, 2]], 0, 0, ["ja"], 2)
+    iota(T.jh[:], [[1, 16], [0, 32]], 0, 0, ["jh"], 512)
+    add("G", lambda: g.affine_select(T.seg[:], T.one[:], [[0, 32], [1, 16]], OP.not_equal, 0.0, 0, 0), 170 + 1024 * CYC, ["one"], ["seg"])
+    ts(T.Tm[:, 0:1], T.pM[:, 64:65], 1023.5, None, OP.add, None, [], ["Tm"], bank=["pM"])
+    ts(T.Lp[:], T.lsi[:], 32.0, None, OP.add, None, ["lsi"], ["Lp0", "Lp1"])
+    act(T.cols[:, 3:4], q, AF.Identity, ["i16a"], ["c3"], 1, scale=2.0, bias=1.0)
+    act(T.cols[:, 4:5], q, AF.Identity, ["i16a"], ["c4"], 1, scale=32.0)
+    act(T.base[:], T.jb[:], AF.Identity, ["jb", "c4"], ["base"], 4, bias=T.cols[:, 4:5])
+    act(T.W5[:], T.W1[:], AF.Identity, ["W1"], ["W5"], 144, scale=512.0)
+    act(T.Wt[:], T.BO[:], AF.Identity, ["BO", "c3"], ["Wt"], 128, scale=T.cols[:, 3:4])
+    act(T.ktab[:], T.jk[:], AF.Identity, ["jk", "i16a"], ["ktab"], 32, bias=q)
+    ts(T.hot[:], T.jh[:], q, 4096.0, OP.not_equal, OP.mult, ["jh", "i16a"], ["hot"], 256)
+    ts(T.rst[:], T.seg[:, 0:64], -65536.0, 65536.0, OP.mult, OP.add, ["seg"], ["rst"])
+    ts(T.gt[:], T.jm[:], q, None, OP.is_gt, None, ["jm", "i16a"], ["gt"])
+    ts(T.pick[:], T.gt[:], 4325376.0, -4194304.0, OP.mult, OP.add, ["gt"], ["pick"])
+    ts(T.cols[:, 7:8], q, 8.0, None, OP.is_ge, None, ["i16a"], ["c7"])
+    ts(T.al[:], T.ja[:], T.cols[:, 7:8], None, OP.add, None, ["ja", "c7"], ["al"])
+    names = lambda k: ["SB%d%s" % (k, x) for x in "wzcpq"]
+    ts(T.SB[:, 0:80, :], T.one[:, 0:400], 0.0, None, OP.mult, None, ["one"], names(0) + names(1), 200)
+    for k in (2, 4):
+        dma("Y", T.SB[:, 40 * k:40 * k + 80, :], T.SB[:, 0:80, :], names(0) + names(1), names(k) + names(k + 1), 2000)
+    at(None)
+
+    def wide(Wm, i):
+        return Wm[:, 15 - i:143 - i]
+
+    def lanes(buf, k, f):
+        o = 40 * k + (8 if f >= 3 else 0)
+        return buf[:, o:o + 32, f]
+
+    def assemble(k, s, out, wr):
+        o, c = 40 * k, 32 * s
+        if s == 0:
+            cp(T.RB[:, o + 24:o + 32, 3:5], T.SB[:, o + 24:o + 32, 3:5], ["SB%dp" % k, "SB%dq" % k], ["RB%d" % k])
+        tt(T.tb[:, c:c + 32], lanes(T.RB, k, 0), lanes(T.RB, k, 3), OP.min, ["RB%d" % k], ["tb%d" % s])
+        tt(out, T.tb[:, c:c + 32], lanes(T.RB, k, 4), OP.max, ["RB%d" % k, "tb%d" % s], wr)
+
+    def anchors(rnd, s, out, wr):
+        k = 2 * rnd + s
+        if s == 0:
+            tt(out, T.RA[:, 8 * rnd:8 * rnd + 4].indirect(T.al[:]), lanes(T.RB, k, 2), OP.add, ["RB%d" % k, "al", "RA%d" % rnd], wr, gat=True)
+        else:
+            cp(out, lanes(T.RB, k, 2), ["RB%d" % k], wr)
+
+    stg = [0]
+    xrd, Xr = ["X"], T.X0[:]
+    for rnd in range(RO):
+        Tb, tbn = (T.Tm[:, 0:1], "Tm") if rnd == 0 else (T.Tb[:, rnd:rnd + 1], "Tb%d" % rnd)
+        for s in range(2):
+            h, k, e = HALF[s], 2 * rnd + s, 512 * s
+            so = 40 * k
+            nm = lambda x: "%s%d" % (x, s)
+            L16, Lp, K = T.L16[:, h:h + 32], T.Lp[:, h:h + 32], T.K[:, h:h + 32]
+            La, Zs, Ei = T.La[:, e:e + 512], T.Zs[:, 2 * e:2 * e + 512], T.Ei[:, e:e + 512]
+            at(16 * (k - 1) + OPT["names"] if s else None)
+            if rnd == 0:
+                zsrc, zn = T.zin[:, h:h + 32], "zin"
+            else:
+                assemble(k - 2, s, L16, [nm("L")])
+                ts(Lp, L16, 32.0, None, OP.add, None, [nm("L")], [nm("Lp")])
+                anchors(rnd - 1, s, K, [nm("K")])
+                zsrc, zn = lanes(T.RB, k - 2, 1), "RB%d" % (k - 2)
+            i0, prn = 0, []
+            for n in (OPT["start"] if k == 0 else (16,)):
+                c, w = 32 * i0, 32 * n
+                parts = range(i0, i0 + n, 4)
+                for i in range(i0, i0 + n):
+                    mm(T.pLa[:, 32 * i:32 * i + 32], rot[i], L16, "pLa", ("la", k, i0), ["Pm%d" % i, nm("L")], 32, (True, True))
+                act(T.La[:, e + c:e + c + w], T.pLa[:, c:c + w], AF.Identity, ["c6"], ["La%d.%d" % (s, x) for x in parts], w, bank=["pLa"],
+                    bias=T.cols[:, 6:7])
+                mm(T.pLi[:, c:c + w], T.one[0:32, 0:128], T.one[0:32, 0:w], "pLi", ("l0", k, i0), ["one"], w, (True, False))
+                for i in range(i0, i0 + n):
+                    mm(T.pLi[:, 32 * i:32 * i + 32], row[i], L16, "pLi", ("li", k, i0), ["Rm%d" % i, nm("L")], 32, "rest")
+                tt(T.pr[:, e + c:e + c + w], T.La[:, e + c:e + c + w], T.pLi[:, c:c + w], OP.mult, ["La%d.%d" % (s, x) for x in parts],
+                   ["pr%d.%d" % (s, x) for x in parts], w, bank=["pLi"])
+                i0 += n
+            for i in range(16):
+                mm(T.pZ[:, i:512:16], rot[i], zsrc, "pZ", ("z", k), ["Pm%d" % i, zn], 32, (True, True))
+            act(Zs, T.pZ[:], AF.Abs, [], [nm("Zs")], 512, bank=["pZ"])
+            piece, i0, eis = [], 0, []
+            for n in (OPT["pieces"] if s == 0 else (16,)):
+                c, w = e + 32 * i0, 32 * n
+                tt(T.Ni[:, c:c + w], K.indirect(T.sl[:, 0:2 * n]), T.pr[:, c:c + w], OP.add,
+                   [nm("K"), "sl"] + ["pr%d.%d" % (s, x) for x in range(i0, i0 + n, 4)], ["Ni%d" % c], w, gat=True)
+                ts(T.Ei[:, c:c + w], T.Ni[:, c:c + w], 5, 2047, OP.arith_shift_right, OP.bitwise_and, ["Ni%d" % c], ["Ei%d" % c], w)
+                cp(T.O[:, c:c + w], T.Ei[:, c:c + w], ["Ei%d" % c], ["O%d" % c], w)
+                piece += ["O%d" % c] * n; eis.append("Ei%d" % c); i0 += n
+            pD, dn = (T.pD0, T.pD1)[s], nm("pD")
+            for i, nj in runs(KINDS[k]):
+                at(16 * k + i)
+                kind, c0, c1 = KINDS[k][i], 8192 * s + 512 * i, 8192 * s + 512 * (i + nj)
+                dN = ["d%d" % (c0 + 512 * j) for j in range(nj)]
+                rN = ["r%d" % (c0 + 512 * j) for j in range(nj)]
+                got = Xr.indirect(T.O[:, e + 32 * i:e + 32 * (i + nj)])
+                if kind == "D":
+                    act(T.d[:, c0:c1], got, AF.Copy, xrd + [piece[i]], dN, 512 * nj, gat=True)
+                    for j in range(nj):
+                        c = c0 + 512 * j
+                        pS, sn = (T.pS0, T.pS1)[stg[0] % 2], "pS%d" % (stg[0] % 2)
+                        mm(pS[:], T.In[:], Zs, sn, ("s", stg[0]), ["In", nm("Zs")], 512)
+                        mm(pS[:], rot[0], T.d[:, c:c + 512], sn, ("s", stg[0]), ["Pm0", dN[j]], 512)
+                        act(T.r[:, c:c + 512], pS[:], AF.Abs, [], [rN[j]], 512, bank=[sn])
+                        mm(pD[:], wide(T.W1, i + j), T.r[:, c:c + 512], dn, ("d", k), ["W1", rN[j]], 512)
+                        stg[0] += 1
+                    continue
+                for j in range(nj):
+                    c = c0 + 512 * j
+                    tt(T.d[:, c:c + 512], Xr.indirect(T.O[:, e + 32 * (i + j):e + 32 * (i + j) + 32]), Zs, OP.subtract,
+                       xrd + [piece[i], nm("Zs")], [dN[j]], 512, gat=True)
+                if kind == "A":
+                    ts(T.r[:, c0:c1], T.d[:, c0:c1], 0.0, None, OP.max, None, dN, rN, 512 * nj, 0.5)
+                else:
+                    act(T.r[:, c0:c1], T.d[:, c0:c1], AF.Abs, dN, rN, 512 * nj)
+                for j in range(nj):
+                    c = c0 + 512 * j
+                    if kind == "A":
+                        mm(pD[:], wide(T.Wn, i + j), T.d[:, c:c + 512], dn, ("d", k), ["Wn", dN[j]], 512)
+                    mm(pD[:], wide(T.W2 if kind == "A" else T.W1, i + j), T.r[:, c:c + 512], dn, ("d", k), ["W2", "W1", rN[j]], 512)
+            at(None)
+            ind = (T.ind0, T.ind1)[s]
+            act(ind[:], pD[:], AF.Sign, [tbn], [nm("ind")], 512, bank=[dn], bias=Tb, scale=-1.0)
+            for m in range(16):
+                mm(T.pM[:, 0:32], wide(T.W5, m), ind[:, :, m, :], "pM", ("c", k), ["W5", nm("ind")], 32)
+            tt(T.key[:, 0:32], T.ktab[:], T.pM[:, 0:32], OP.subtract, ["ktab"], ["keyt"], bank=["pM"])
+            tt(T.key[:, 32:64], T.ktab[:], T.pM[:, 0:32], OP.add, ["ktab"], ["keyb"], bank=["pM"])
+            scan(T.ksc[:, s, :], T.rst[:], T.key[:], OP.add, OP.min, ["rst", "keyt", "keyb"], [nm("ksc")], 64)
+            if s == 1:
+                pri[0] = 2 * NOW
+                Ac = T.Ac[:, 4 * rnd:4 * rnd + 1]
+                ts(T.ia[:], T.ksc[:, :, 15:32:16], 7680.0, 32.0, OP.is_lt, OP.mult, ["ksc0", "ksc1"], ["ia"])
+                mm(T.pM[:, 64:68], T.BO[:], T.ia[:], "pM", ("a", k), ["BO", "ia"], 4, (True, True))
+                add("V", lambda Ac=Ac: V.tensor_reduce(Ac, T.pM[:, 64:68], AxisListType.X, OP.add), vc(4), (), ["Ac%d" % rnd], [("pM", "V")])
+                message(3 * rnd + 2, DISTS[0][:4], lambda j: Ac, lambda j: T.RA[:, 8 * rnd + j:8 * rnd + j + 1], True,
+                        ["Ac%d" % rnd], ["RA%d" % rnd])
+                if rnd + 1 < RO:
+                    at(16 * k + 20)
+                    ts(T.Ai[:, 0:1], Ac, 1.0 / 32, None, OP.mult, None, ["Ac%d" % rnd], ["Ai0"])
+                    ts(T.Ai[:, 4:5], T.Ai[:, 0:1], 31, None, OP.bitwise_and, None, ["Ai0"], ["Ai1"])
+                    ts(T.Tb[:, rnd + 1:rnd + 2], T.Ai[:, 4:5], T.Tm[:, 0:1], None, OP.add, None, ["Ai1", "Tm"], ["Tb%d" % (rnd + 1)])
+            at(None)
+            cp(T.ki[:, 0:4], T.ksc[:, s, 15:64:16], [nm("ksc")], ["ki0"])
+            ts(T.ki[:, 4:8], T.ki[:, 0:4], 511, None, OP.bitwise_and, None, ["ki0"], ["ki1"])
+            cp(T.ok[:], T.ki[:, 4:8], ["ki1"], ["ok"])
+            tt(T.pw[:], La.indirect(T.ok[:, 0:2]), Lp, OP.mult, ["La%d.%d" % (s, x) for x in (0, 4, 8, 12)] + ["ok", nm("Lp")], ["pw"], gat=True)
+            tt(T.nw[:], T.pw[:], K, OP.add, ["pw", nm("K")], ["nw"])
+            ts(T.wi[:], T.nw[:], 5, 2047, OP.arith_shift_right, OP.bitwise_and, ["nw"], ["wi"])
+            cp(T.ow[:], T.wi[:], ["wi"], ["ow"])
+            cp(lanes(T.SB, k, 0), T.wi[:], ["wi"], ["SB%dw" % k])
+            cp(lanes(T.SB, k, 3), T.hot[:].indirect(T.ok[:, 2:4]), ["hot", "ok"], ["SB%dq" % k], c=gc_(32, 50))
+            tt(lanes(T.SB, k, 4), Ei.indirect(T.ok[:, 0:2]), lanes(T.SB, k, 3), OP.subtract, eis + ["ok", "SB%dq" % k], ["SB%dp" % k], gat=True)
+            cut = OPT["split"] if s else 512
+            act(T.Gb[:, 0:cut], Xr.indirect(T.ow[:, 0:cut // 16]), AF.Copy, xrd + ["ow"], ["Gb0"], cut, gat=True)
+            if cut < 512:
+                cp(T.Gb[:, cut:512], Xr.indirect(T.ow[:, cut // 16:32]), xrd + ["ow"], ["Gb1"], c=gc_(512 - cut, 50))
+            scan(T.Mx[:], T.seg[:], T.Gb[:], OP.mult, OP.max, ["seg", "Gb0", "Gb1"], ["Mx"], 256)
+            M, z0, Y = T.Mx[:, 15:512:16], T.Zs[:, 2 * e:2 * e + 512:16], T.Y[:, h:h + 32]
+            tt(T.sm[:], M, z0, OP.add, ["Mx", nm("Zs")], ["sm"])
+            ts(T.Yi[:], T.sm[:], 0.5, -0.25, OP.mult, OP.add, ["sm"], ["Yi"])
+            cp(Y, T.Yi[:], ["Yi"], [nm("Y")])
+            tt(lanes(T.SB, k, 1), z0, M, OP.subtract, ["Mx", nm("Zs")], ["SB%dz" % k])
+            mm(T.pM[:, 128 + h:160 + h], T.Wt[:], Y, "pM", ("u", k), ["Wt", nm("Y")], 32, (True, True))
+            if s == 1:
+                pri[0] = NOW + (OPT["write"] if rnd + 1 < RO else -2e4)
+                scan(T.us[:], T.pick[:], T.pM[:, 128:192], OP.add, OP.max, ["pick"], ["us"], 64, bank=["pM"])
+                cp(T.u31[:, 0:4], T.us[:, 15:64:16], ["us"], ["u30"])
+                ts(T.u31[:, 4:8], T.u31[:, 0:4], 31, None, OP.bitwise_and, None, ["u30"], ["u31"])
+                tt(T.u31[:, 8:12], T.u31[:, 4:8], T.base[:], OP.add, ["u31", "base"], ["u32"])
+                cp(T.pl[:], T.u31[:, 8:12], ["u32"], ["pl"])
+                cp(Xr.indirect(T.pl[:]), T.Y[:], ["pl", "Y0", "Y1"], ["X"], c=50 + 64 * 4 * CYC)
+                at(None)
+            cp(T.ui[:], T.pM[:, 128 + h:160 + h], [], ["ui"], bank=["pM"])
+            ts(T.um[:], T.ui[:], 2047, None, OP.bitwise_and, None, ["ui"], ["um"])
+            ts(T.ut[:], T.um[:], 1184.0, None, OP.add, None, ["um"], ["ut"])
+            tt(T.up[:], T.um[:], T.ut[:], OP.mult, ["um", "ut"], ["up"])
+            ts(T.uc[:], T.up[:], 65504, None, OP.bitwise_and, None, ["up"], ["uc"])
+            if s == 0:
+                ts(lanes(T.SB, k, 2), T.uc[:], -64512.0, None, OP.add, None, ["uc"], ["SB%dc" % k])
+            else:
+                ts(lanes(T.SB, k, 2), T.uc[:], -64512.0, Ac, OP.add, OP.add, ["uc", "Ac%d" % rnd], ["SB%dc" % k])
+            message(3 * rnd + s, DISTS[s], lambda j: T.SB[:, so + 8 * j:so + 8 * j + 8, :], lambda j: T.RB[:, so + 8 * j:so + 8 * j + 8, :],
+                    False, names(k), ["RB%d" % k], ahead=["SB%dp" % k, "SB%dq" % k] if s else None)
+    dma("Y", T.yx[:, 0:W // 2], T.X0[:, 0:W // 2], xrd, (), 3500)
+    dma("S", T.yx[:, W // 2:W], T.X0[:, W // 2:W], xrd, (), 3500)
+
+    for s in range(2):
+        h, k = HALF[s], 2 * (RO - 1) + s
+        at(None if s else 200)
+        assemble(k, s, T.oL[:, h:h + 32], ["oL%d" % s])
+        dz = lanes(T.RB, k, 1)
+        ts(T.on[:, h:h + 32], dz, -1.0, None, OP.mult, None, ["RB%d" % k], ["on%d" % s])
+        tt(T.oz[:, h:h + 32], T.on[:, h:h + 32], dz, OP.max, ["RB%d" % k, "on%d" % s], ["oz%d" % s])
+        if s == 0:
+            anchors(RO - 1, s, T.Kc[:], ["Kc"])
+            ts(T.oi[:, h:h + 32], T.Kc[:], -1024.0, None, OP.add, None, ["Kc"], ["oi0"])
+        else:
+            ts(T.oi[:, h:h + 32], lanes(T.RB, k, 2), -1024.0, None, OP.add, None, ["RB%d" % k], ["oi1"])
+        ts(T.oj[:, h:h + 32], T.oi[:, h:h + 32], 5, 2047, OP.arith_shift_right, OP.bitwise_and, ["oi%d" % s], ["oj%d" % s])
+        cp(T.oa[:, h:h + 32], T.oj[:, h:h + 32], ["oj%d" % s], ["oa%d" % s])
+    dma("Y", T.yl[:], T.oL[:], ["oL0", "oL1"], (), 2000)
+    dma("S", T.yz[:], T.oz[:], ["oz0", "oz1"], (), 2000)
+    dma("Y", T.ya[:], T.oa[0:128:16, :], ["oa0", "oa1"], (), 2000)
+
+    n = len(ops)
+    users = [[] for _ in range(n)]
+    for o in ops:
+        for x in o["dep"]:
+            users[x].append(o["n"])
+    way = [0.0] * n
+    for o in reversed(ops):
+        way[o["n"]] = o["cost"] + o["lat"] + max([way[u] + LAT for u in users[o["n"]]] + [0.0])
+    for o in ops:
+        way[o["n"]] += o["pri"]
+    left = [len(o["dep"]) for o in ops]
+    ready, done = [0.0] * n, [0.0] * n
+    free = {e: 0.0 for e in queue}
+    cand = [o["n"] for o in ops if not o["dep"]]
+    plan = repr((n, KINDS, OPT))
+    order = ORDER.get(plan, [])
+    if order:
+        cand = []
+    ORDER[plan] = order
+    while cand:
+        est = {x: max(ready[x], free.get(ops[x]["eng"], 0.0)) for x in cand}
+        x0 = min(cand, key=lambda x: (est[x], -way[x], x))
+        e = ops[x0]["eng"]
+        mine = [y for y in cand if ops[y]["eng"] == e]
+        x = max((y for y in mine if est[y] <= est[x0] + OPT["look"]), key=lambda y: (way[y], -y))
+        if est[x] > est[x0] + OPT["gap"]:
+            short = [y for y in mine if est[y] <= est[x0] + 1 and ops[y]["cost"] <= 115]
+            if short:
+                x = max(short, key=lambda y: (way[y], -y))
+        cand.remove(x); order.append(x)
+        if e is not None:
+            free[e] = est[x] + ops[x]["cost"]
+        done[x] = est[x] + ops[x]["cost"] + ops[x]["lat"]
+        for u in users[x]:
+            ready[u] = max(ready[u], done[x] + (0.0 if e == "P" and ops[u]["eng"] == "P" else LAT))
+            left[u] -= 1
+            if left[u] == 0:
+                cand.append(u)
+
+    pos = {x: j for j, x in enumerate(order)}
+    seen, waits, marked = {}, {}, set()
+    for x in order:
+        o = ops[x]
+        if o["eng"] is None:
+            continue
+        need, w = {}, []
+        for y in o["dep"]:
+            p = ops[y]
+            if p["kind"] == "s" or (p["eng"] == "P" and o["eng"] == "P"):
+                continue
+            key = p["sem"][0] if p["sem"] else p["eng"]
+            if key not in need or pos[y] > pos[need[key]]:
+                need[key] = y
+        for key in sorted(need):
+            y = need[key]
+            if seen.get((o["eng"], key), -1) < pos[y]:
+                seen[(o["eng"], key)] = pos[y]; w.append(y); marked.add(y)
+        waits[x] = w
+    count, val = {}, {}
+    size, met = {}, {}
+    for o in ops:
+        size[o["grp"]] = size.get(o["grp"], 0) + 1
+    tail = []
+    for x in order:
+        o = ops[x]
+        if o["eng"] is None:
+            continue
+        qu = queue[o["eng"]]
+        for y in waits[x]:
+            s, v = ops[y]["sem"] or (ops[y]["eng"], val[y])
+            qu.wait_ge(T.sem[s], v)
+        if "mm" in o:
+            out, lhsT, rhs, flags = o["mm"]
+            met[o["grp"]] = met.get(o["grp"], 0) + 1
+            last = met[o["grp"]] == size[o["grp"]]
+            if flags is None:
+                flags = (met[o["grp"]] == 1, last)
+            elif flags == "rest":
+                flags = (False, last)
+            ins = P.matmul(out, lhsT, rhs, flags[0], flags[1])
+        else:
+            ins = o["fn"]()
+        if o["kind"] == "d":
+            ins.then_inc(T.sem[o["sem"][0]], 16)
+            if x not in marked:
+                tail.append((qu, o["sem"]))
+        elif x in marked:
+            count[o["eng"]] = count.get(o["eng"], 0) + 1
+            val[x] = count[o["eng"]]
+            ins.then_inc(T.sem[o["eng"]], 1)
+    for qu, (s, v) in tail:
+        qu.wait_ge(T.sem[s], v)
+    g.wait_ge(T.sem.sent, sent[0])

@@ -4,8 +4,8 @@ from concourse.mybir import AluOpType as OP, AxisListType, ActivationFunctionTyp
 NR, RO, W = 8, 3, 2048
 HALF = (32, 0)
 DISTS = ((5, 6, 7, 1, 2), (1, 2, 3, 4, 5))
-KINDS = ["AADADDAADDDADAAD", "DDAADDAADDABDDBA"] + ["DDAADDAADDAAADAD", "DBDDBDAADDBBDABA"] * 2
-OPT = {"names": 5, "late": 10, "look": 90.0, "rmv": 6, "split": 256, "pieces": (4, 4, 8), "gap": 30.0, "start": (4, 4, 8), "write": 3000.0}
+KINDS = ["GGAAGGAAGGAAGGAA", "GGGGGGGHAAHHDADD"] + ["GGGGAAAAHHGGAAAA", "GGGGBGGGAAHHDDAD"] * 2
+OPT = {"names": 2, "late": 10, "look": 90.0, "rmv": 6, "split": 256, "pieces": (4, 4, 8), "gap": 10.0, "start": (4, 4, 8), "write": 3000.0, "add": 4000.0}
 ORDER = {}
 
 F, B, H, I, U = "float32", "bfloat16", "float16", "int32", "uint16"
@@ -41,7 +41,7 @@ SCRATCH = {
     "pD0": ("psum", [128, 512], F), "pD1": ("psum", [128, 512], F), "pS0": ("psum", [128, 512], F), "pS1": ("psum", [128, 512], F),
     "pLa": ("psum", [128, 512], F), "pLi": ("psum", [128, 512], F), "pZ": ("psum", [128, 512], F), "pM": ("psum", [128, 512], F),
 }
-NDMA = 12
+NDMA = 90
 SEMAPHORES = ["V", "S", "P", "G", "sent"] + ["dma%d" % k for k in range(NDMA)] + ["arr%d" % k for k in range(3 * RO)]
 
 CYC, PEC, GAT, LAT = 1.04, 0.52, 1.56, 70.0
@@ -282,6 +282,8 @@ def rank_program(g, core, T, topo):
             for i in range(16):
                 mm(T.pZ[:, i:512:16], rot[i], zsrc, "pZ", ("z", k), ["Pm%d" % i, zn], 32, (True, True))
             act(Zs, T.pZ[:], AF.Abs, [], [nm("Zs")], 512, bank=["pZ"])
+            if "GG" in KINDS[k] or "HH" in KINDS[k]:
+                dma("Y", T.Zs[:, 2 * e + 512:2 * e + 1024], Zs, [nm("Zs")], [nm("Zt")], 2500)
             piece, i0, eis = [], 0, []
             for n in (OPT["pieces"] if s == 0 else (16,)):
                 c, w = e + 32 * i0, 32 * n
@@ -308,19 +310,23 @@ def rank_program(g, core, T, topo):
                         mm(pD[:], wide(T.W1, i + j), T.r[:, c:c + 512], dn, ("d", k), ["W1", rN[j]], 512)
                         stg[0] += 1
                     continue
-                for j in range(nj):
-                    c = c0 + 512 * j
-                    tt(T.d[:, c:c + 512], Xr.indirect(T.O[:, e + 32 * (i + j):e + 32 * (i + j) + 32]), Zs, OP.subtract,
-                       xrd + [piece[i], nm("Zs")], [dN[j]], 512, gat=True)
-                if kind == "A":
+                if kind in "GH":
+                    act(T.d[:, c0:c1], got, AF.Identity, xrd + [piece[i]], dN, 512 * nj, gat=True, scale=-1.0)
+                    dma("G", T.d[:, c0:c1], T.Zs[:, 2 * e:2 * e + 512 * nj], [nm("Zs"), nm("Zt")], dN, OPT["add"], 1000.0, accum_op=OP.add)
+                else:
+                    for j in range(nj):
+                        c = c0 + 512 * j
+                        tt(T.d[:, c:c + 512], Xr.indirect(T.O[:, e + 32 * (i + j):e + 32 * (i + j) + 32]), Zs, OP.subtract,
+                           xrd + [piece[i], nm("Zs")], [dN[j]], 512, gat=True)
+                if kind in "AG":
                     ts(T.r[:, c0:c1], T.d[:, c0:c1], 0.0, None, OP.max, None, dN, rN, 512 * nj, 0.5)
                 else:
                     act(T.r[:, c0:c1], T.d[:, c0:c1], AF.Abs, dN, rN, 512 * nj)
                 for j in range(nj):
                     c = c0 + 512 * j
-                    if kind == "A":
+                    if kind in "AG":
                         mm(pD[:], wide(T.Wn, i + j), T.d[:, c:c + 512], dn, ("d", k), ["Wn", dN[j]], 512)
-                    mm(pD[:], wide(T.W2 if kind == "A" else T.W1, i + j), T.r[:, c:c + 512], dn, ("d", k), ["W2", "W1", rN[j]], 512)
+                    mm(pD[:], wide(T.W2 if kind in "AG" else T.W1, i + j), T.r[:, c:c + 512], dn, ("d", k), ["W2", "W1", rN[j]], 512)
             at(None)
             ind = (T.ind0, T.ind1)[s]
             act(ind[:], pD[:], AF.Sign, [tbn], [nm("ind")], 512, bank=[dn], bias=Tb, scale=-1.0)

@@ -4,45 +4,49 @@ from concourse.mybir import AluOpType as OP, AxisListType, ActivationFunctionTyp
 NR, RO, W = 8, 3, 2048
 HALF = (32, 0)
 DISTS = ((5, 6, 7, 1, 2), (1, 2, 3, 4, 5))
-KINDS = ["GGAAGGAAGGAAGGAA", "GGGGGGGHAAHHDADD"] + ["GGGGAAAAHHGGAAAA", "GGGGBGGGAAHHDDAD"] * 2
-OPT = {"names": 2, "late": 10, "look": 90.0, "rmv": 6, "split": 256, "pieces": (4, 4, 8), "gap": 10.0, "start": (4, 4, 8), "write": 3000.0, "add": 4000.0}
-ORDER = {}
+KINDS = ["GGAAFFAAGAAADDGA", "FFFFFFAAGGDAGGDD"] + ["FFAAFFFFAAGGAADA", "FFFFFFGGAAGAGAAD"] * 2
+OPT = {"names": 0, "late": 10, "look": 90.0, "rmv": 4, "split": 256, "pieces": (4, 4, 8), "gap": 10.0, "start": (4, 4, 8), "write": 3000.0,
+       "add": 2000.0, "msg": (5500.0, 5000.0, 4300.0), "sg": 1024, "vr": 512, "cut4": 3, "last": (8, 8), "c4": "VS",
+       "passes": 3, "fold": 5200.0, "va": 16, "tries": [(a, b, c) for a in (0.0, 90.0, 200.0) for b in (0.0, 200.0) for c in (40.0, 120.0)], "shake": 600.0, "early": (8, 8), "lead": 1000.0,
+       "row": 30.0, "rate": 25.0, "vv": 90.0}
+ORDER, PLAN = {}, [0.0]
 
 F, B, H, I, U = "float32", "bfloat16", "float16", "int32", "uint16"
 SCRATCH = {
-    "X0": ("sbuf", [128, W], B), "jb": ("sbuf", [128, 4], F), "base": ("sbuf", [128, 4], F),
+    "X0": ("sbuf", [128, W + 64], B), "Nm": ("sbuf", [128, 16, 32], I), "vi": ("sbuf", [128, 64], I), "jb": ("sbuf", [128, 4], F), "base": ("sbuf", [128, 4], F),
     "lsi": ("sbuf", [128, 64], I), "zin": ("sbuf", [128, 64], B), "ani": ("sbuf", [128, 72], I), "anh": ("sbuf", [128, 72], H),
     "jc": ("sbuf", [128, 144], B), "jg": ("sbuf", [128, 128], B), "jm": ("sbuf", [128, 64], F), "ja": ("sbuf", [128, 2], F),
-    "jh": ("sbuf", [128, 512], B), "jk": ("sbuf", [128, 32], F), "jl": ("sbuf", [128, 32], F), "jp": ("sbuf", [128, 20], I),
+    "jh": ("sbuf", [128, 512], B), "jk": ("sbuf", [128, 32], F), "jp": ("sbuf", [128, 20], I),
     "pq": ("sbuf", [128, 20], I), "cols": ("sbuf", [128, 32], F), "i16": ("sbuf", [128, 16], F),
     "Pm": ("sbuf", [128, 2048], B), "Rm": ("sbuf", [128, 2048], B),
     "BO": ("sbuf", [128, 128], B), "Wt": ("sbuf", [128, 128], B), "In": ("sbuf", [128, 128], B),
-    "W1": ("sbuf", [128, 144], B), "W2": ("sbuf", [128, 144], B), "Wn": ("sbuf", [128, 144], B), "W5": ("sbuf", [128, 144], B),
+    "W8": ("sbuf", [128, 24], B), "Wc": ("sbuf", [128, 288], B), "Sel": ("sbuf", [128, 512], B), "TB": ("sbuf", [128, 128], H),
+    "ind": ("sbuf", [128, 512], B), "C4": ("sbuf", [128, 128], B),
     "one": ("sbuf", [128, 512], B), "seg": ("sbuf", [128, 512], B), "rst": ("sbuf", [128, 64], F),
     "gt": ("sbuf", [128, 64], F), "pick": ("sbuf", [128, 64], F), "al": ("sbuf", [128, 2], U),
-    "hot": ("sbuf", [128, 512], B), "ktab": ("sbuf", [128, 32], F), "sl": ("sbuf", [128, 32], U),
+    "hot": ("sbuf", [128, 512], B), "ktab": ("sbuf", [128, 32], F),
     "SB": ("sbuf", [128, 240, 5], H), "RB": ("sbuf", [128, 240, 5], H), "RA": ("sbuf", [128, 24], F),
     "Tm": ("sbuf", [128, 4], F), "Tb": ("sbuf", [128, 4], F), "Ac": ("sbuf", [128, 12], F),
     "Ai": ("sbuf", [128, 8], I),
-    "L16": ("sbuf", [128, 64], H), "Lp": ("sbuf", [128, 64], F), "K": ("sbuf", [128, 64], F), "Kc": ("sbuf", [128, 32], F),
+    "L16": ("sbuf", [128, 64], H), "Lp": ("sbuf", [128, 64], F), "K": ("sbuf", [128, 64], H), "Kc": ("sbuf", [128, 32], F),
     "ta": ("sbuf", [128, 64], F), "tb": ("sbuf", [128, 64], F),
     "La": ("sbuf", [128, 1024], F), "Zs": ("sbuf", [128, 2048], B), "pr": ("sbuf", [128, 1024], F),
-    "Ni": ("sbuf", [128, 1024], I), "Ei": ("sbuf", [128, 1024], I), "O": ("sbuf", [128, 1024], U),
+    "Ni": ("sbuf", [128, 1024], I), "Ei": ("sbuf", [128, 1024], I), "O": ("sbuf", [128, 1024], U), "Oa": ("sbuf", [128, 16, 32], U),
     "d": ("sbuf", [128, 16384], B), "r": ("sbuf", [128, 16384], B),
-    "ind0": ("sbuf", [128, 2, 16, 16], B), "ind1": ("sbuf", [128, 2, 16, 16], B),
     "key": ("sbuf", [128, 64], F), "ksc": ("sbuf", [128, 2, 64], F), "ki": ("sbuf", [128, 8], I), "ok": ("sbuf", [128, 4], U),
     "ia": ("sbuf", [128, 4], B), "pw": ("sbuf", [128, 32], F), "nw": ("sbuf", [128, 32], I), "wi": ("sbuf", [128, 32], I),
-    "ow": ("sbuf", [128, 32], U), "wh": ("sbuf", [128, 32], F), "Gb": ("sbuf", [128, 512], B), "Mx": ("sbuf", [128, 512], B),
-    "sm": ("sbuf", [128, 32], F), "Yi": ("sbuf", [128, 32], I), "Y": ("sbuf", [128, 64], B), "ui": ("sbuf", [128, 32], I),
+    "ow": ("sbuf", [128, 32], U), "Gb": ("sbuf", [128, 512], B), "Mx": ("sbuf", [128, 512], B),
+    "zh": ("sbuf", [128, 64], F), "Yi": ("sbuf", [128, 32], I), "Y": ("sbuf", [128, 64], B), "ui": ("sbuf", [128, 32], I),
     "um": ("sbuf", [128, 32], I), "ut": ("sbuf", [128, 32], F), "up": ("sbuf", [128, 32], I), "uc": ("sbuf", [128, 32], I),
     "us": ("sbuf", [128, 64], F), "u31": ("sbuf", [128, 12], I), "pl": ("sbuf", [128, 4], U),
-    "oL": ("sbuf", [128, 64], F), "oz": ("sbuf", [128, 64], B), "on": ("sbuf", [128, 64], F), "oi": ("sbuf", [128, 64], I),
+    "oL": ("sbuf", [128, 64], F), "oz": ("sbuf", [128, 64], B), "oi": ("sbuf", [128, 64], I),
     "oj": ("sbuf", [128, 64], I), "oa": ("sbuf", [128, 64], F),
     "pD0": ("psum", [128, 512], F), "pD1": ("psum", [128, 512], F), "pS0": ("psum", [128, 512], F), "pS1": ("psum", [128, 512], F),
     "pLa": ("psum", [128, 512], F), "pLi": ("psum", [128, 512], F), "pZ": ("psum", [128, 512], F), "pM": ("psum", [128, 512], F),
 }
-NDMA = 90
-SEMAPHORES = ["V", "S", "P", "G", "sent"] + ["dma%d" % k for k in range(NDMA)] + ["arr%d" % k for k in range(3 * RO)]
+NDMA, NFOLD = 90, 32
+SEMAPHORES = (["V", "S", "P", "G", "sent"] + ["dma%d" % k for k in range(NDMA)] + ["arr%d" % k for k in range(3 * RO)] +
+              ["fold%d" % k for k in range(NFOLD)])
 
 CYC, PEC, GAT, LAT = 1.04, 0.52, 1.56, 70.0
 NOW = 1e9
@@ -69,18 +73,124 @@ def calls_for(src, dsts, topo, same, apart):
     return ahead + [call]
 
 
+def first_order(ops, users, look, far, short_):
+    n = len(ops)
+    way = [0.0] * n
+    for o in reversed(ops):
+        way[o["n"]] = o["cost"] + o["lat"] + max([way[u] + LAT for u in users[o["n"]]] + [0.0])
+    for o in ops:
+        way[o["n"]] += o["pri"]
+    left = [len(o["dep"]) for o in ops]
+    ready, free, order = [0.0] * n, {}, []
+    cand = [o["n"] for o in ops if not o["dep"]]
+    while cand:
+        est = {x: max(ready[x], free.get(ops[x]["eng"], 0.0)) for x in cand}
+        x0 = min(cand, key=lambda x: (est[x], -way[x], x))
+        e = ops[x0]["eng"]
+        mine = [y for y in cand if ops[y]["eng"] == e]
+        x = max((y for y in mine if est[y] <= est[x0] + look), key=lambda y: (way[y], -y))
+        soon = [y for y in mine if ops[y]["pri"] > 0 and est[y] <= est[x0] + far]
+        if soon:
+            x = max(soon, key=lambda y: (way[y], -y))
+        if est[x] > est[x0] + OPT["gap"]:
+            short = [y for y in mine if est[y] + ops[y]["cost"] <= est[x] + short_]
+            if short:
+                x = max(short, key=lambda y: (way[y], -y))
+        cand.remove(x); order.append(x)
+        if e is not None:
+            free[e] = est[x] + ops[x]["cost"]
+        for u in users[x]:
+            ready[u] = max(ready[u], est[x] + ops[x]["cost"] + ops[x]["lat"] + (0.0 if e == "P" and ops[u]["eng"] == "P" else LAT))
+            left[u] -= 1
+            if left[u] == 0:
+                cand.append(u)
+    return order
+
+
+def place(ops, before, after, lag, rank_of, back):
+    n = len(ops)
+    left = [len(before[x]) for x in range(n)]
+    start, busy = [0.0] * n, {}
+    ready = [ops[x]["lat"] if back else 0.0 for x in range(n)]
+    cand = {x for x in range(n) if not left[x]}
+    end = 0.0
+    while cand:
+        x = min(cand, key=lambda y: (rank_of[y], y))
+        cand.remove(x)
+        o = ops[x]
+        holds = [(o["eng"], 0.0, o["cost"])] if o["eng"] else []
+        if o["use"]:
+            holds.append(("Q", -o["use"] - OPT["lead"] if back else o["cost"] + OPT["lead"], o["use"]))
+        t, moved = ready[x], True
+        while moved:
+            moved = False
+            for e, off, dur in holds:
+                for a, b in busy.get(e, ()):
+                    if b <= t + off + 1e-3:
+                        continue
+                    if a >= t + off + dur - 1e-3:
+                        break
+                    t, moved = b - off, True
+        for e, off, dur in holds:
+            line = busy.setdefault(e, [])
+            j = len(line)
+            while j and line[j - 1][0] > t + off:
+                j -= 1
+            line.insert(j, (t + off, t + off + dur))
+        start[x] = t
+        end = max(end, t + o["cost"] + (0.0 if back else o["lat"]))
+        for u in after[x]:
+            ready[u] = max(ready[u], t + o["cost"] + (lag(u, x) if back else lag(x, u)))
+            left[u] -= 1
+            if not left[u]:
+                cand.add(u)
+    return start, end
+
+
+def tighten(ops, users, order):
+    n = len(ops)
+    deps = [sorted(o["dep"]) for o in ops]
+    lag = lambda a, b: ops[a]["lat"] + (0.0 if ops[a]["eng"] == "P" and ops[b]["eng"] == "P" or ops[a]["kind"] == "s" else
+                                      OPT["vv"] if ops[a]["eng"] == ops[b]["eng"] == "V" else LAT)
+    rank_of = [0.0] * n
+    for j, x in enumerate(order):
+        rank_of[x] = j
+    best, seed = None, 1
+    for t in range(OPT["passes"]):
+        start, end = place(ops, deps, users, lag, rank_of, False)
+        if best is None or end < best[0]:
+            best = (end, start)
+        elif t % 2:
+            start = []
+            for x in range(n):
+                seed = (seed * 1103515245 + 12345) % 2147483648
+                start.append(best[1][x] + OPT["shake"] * seed / 2147483648)
+        start, end = place(ops, users, deps, lag, [-(start[x] + ops[x]["cost"]) for x in range(n)], True)
+        rank_of = [-(start[x] + ops[x]["cost"]) for x in range(n)]
+    return best[0], sorted(range(n), key=lambda x: (best[1][x], x))
+
+
 def rank_program(g, core, T, topo):
+    aide = {c: [x for x in topo.cores_of(c) if topo.die(x) == topo.die(c) and x not in T.cores][0] for c in T.cores}
+    me = core
+    if T.rank_of(core) is None:
+        if core not in aide.values() or not any("F" in x for x in KINDS):
+            return
+        core = [c for c in T.cores if aide[c] == me][0]
     rank = T.rank_of(core)
-    if rank is None:
-        return
+    folds = []
     V, S, P = g.vector, g.scalar, g.tensor
     queue = {"V": V, "S": S, "P": P, "G": g, "Y": g.sync}
     ops, reg, ndma, sent, pri = [], {}, [0], [0], [NOW]
 
     def add(eng, fn, cost, rd=(), wr=(), bank=(), kind="c", lat=0.0, after=(), sem=None):
         o = {"n": len(ops), "eng": eng, "fn": fn, "cost": cost, "kind": kind, "lat": lat, "dep": set(after), "sem": sem, "grp": None,
-             "pri": pri[0]}
-        acc = [(x, "r") for x in rd] + [(x, None) for x in wr] + list(bank)
+             "pri": pri[0], "use": 0.0}
+        link(o, [(x, "r") for x in rd] + [(x, None) for x in wr] + list(bank))
+        ops.append(o)
+        return o["n"]
+
+    def link(o, acc):
         for x, tag in acc:
             cur, prev = reg.get(x, ((None, []), []))
             if tag is not None and cur[0] == tag:
@@ -88,8 +198,6 @@ def rank_program(g, core, T, topo):
             else:
                 o["dep"].update(cur[1]); reg[x] = ((tag, [o["n"]]), cur[1])
         o["dep"].discard(o["n"])
-        ops.append(o)
-        return o["n"]
 
     def at(chunk):
         pri[0] = NOW if chunk is None else -1e6 * chunk
@@ -100,12 +208,12 @@ def rank_program(g, core, T, topo):
     def gc_(n, base):
         return base + n * GAT * CYC
 
-    def ts(out, in0, s1, s2, op0, op1, rd, wr, n=32, f=1.0, bank=()):
+    def ts(out, in0, s1, s2, op0, op1, rd, wr, n=32, f=1.0, bank=(), c=None):
         if op1 is None:
             fn = lambda: V.tensor_scalar(out, in0, s1, None, op0)
         else:
             fn = lambda: V.tensor_scalar(out, in0, s1, s2, op0, op1)
-        return add("V", fn, vc(n, f), rd, wr, [(b, "V") for b in bank])
+        return add("V", fn, c or vc(n, f), rd, wr, [(b, "V") for b in bank])
 
     def tt(out, a, b, op, rd, wr, n=32, bank=(), gat=False):
         c = gc_(n, 50) if gat else vc(n, 1.0 if bank else 2.0)
@@ -124,13 +232,22 @@ def rank_program(g, core, T, topo):
         return add("S", lambda: S.activation(out, a, func, **kw), gc_(n, 65) if gat else vc(n), rd, wr, [(x, "S") for x in bank])
 
     def mm(out, lhsT, rhs, bank, tag, rd, n, flags=None):
-        k = add("P", None, max(64, n) * PEC, rd, (), [(bank, tag)])
-        ops[k]["mm"] = (out, lhsT, rhs, flags); ops[k]["grp"] = (bank, tag)
-        return k
+        o = ops[-1]
+        if n <= 64 and o["grp"] == (bank, tag) and len(o["mm"]) < 4 and o["cost"] == 64 * PEC * len(o["mm"]):
+            link(o, [(x, "r") for x in rd])
+            o["cost"] = 64 * PEC * (len(o["mm"]) + 1)
+        else:
+            o = ops[add("P", None, max(64, n) * PEC, rd, (), [(bank, tag)])]
+            o["mm"] = []; o["grp"] = (bank, tag)
+        o["mm"].append((out, lhsT, rhs, flags))
 
-    def dma(eng, out, a, rd, wr, lat, cost=60.0, **kw):
+    def dma(eng, out, a, rd, wr, lat, cost=60.0, size=0, **kw):
         s = "dma%d" % ndma[0]; ndma[0] += 1
-        return add(eng, lambda: queue[eng].dma_start(out, a, **kw), cost, rd, wr, kind="d", lat=lat, sem=(s, 16))
+        x = add(eng, lambda: queue[eng].dma_start(out, a, **kw), cost, rd, wr, kind="d", lat=lat, sem=(s, 16))
+        if size:
+            ops[x]["use"] = (128 * OPT["row"] + size / OPT["rate"]) / 16
+            ops[x]["lat"] = lat + ops[x]["use"]
+        return x
 
     def iota(out, pat, base, cm, wr, n, small=True):
         if small:
@@ -153,24 +270,38 @@ def rank_program(g, core, T, topo):
                 sent[0] += len(es)
             made.append(add("G", lambda tr=tr: g.remote_dma_fused(tr, local_sem=T.sem.sent), 500.0,
                             rd if call is calls[-1] else ahead, (), kind="s"))
+            ops[made[-1]]["use"] = OPT["row"] * (48 if same else 64 if call is calls[-1] else 16)
         total = 0
         for j, x in enumerate(dists):
             s = (rank - x) % NR
             for call in calls_for(T.cores[s], [T.cores[(s + y) % NR] for y in dists], topo, same, ahead is not None):
                 total += sum(len(es) for js, es in call if j in js)
-        add(None, None, 0.0, (), wr, kind="a", lat=4000.0 if same else 4600.0, after=made, sem=(arr, total))
+        add(None, None, 0.0, (), wr, kind="a", lat=OPT["msg"][no % 3], after=made, sem=(arr, total))
 
-    fill(T.ani[:], 0, ["ani", "thi"], 72)
+    def fold(a, b, out, n, rd, wr):
+        at_ = sum(x[2] for x in folds)
+        land = (T.d if at_ < 16384 else T.r)[:, at_ % 16384:at_ % 16384 + n]
+        sem, mask = "fold%d" % len(folds), topo.mask(core, aide[core])
+        rid, pnc = topo.addr(aide[core], core)
+        tr = [RemoteDMATransfer(dst_ids=[DstId(rid=rid, pnc=pnc)], dma_engine_mask=mask, remote_sem=T.sem[sem], srcs=[a, b], dsts=[land], alu_op=2)]
+        many = len(topo.engines(core, aide[core]))
+        sent[0] += many
+        made = add("G", lambda: g.remote_dma_fused(tr, local_sem=T.sem.sent), 600.0, rd, wr, kind="s")
+        use = (128 * OPT["row"] + 256 * n / OPT["rate"]) / 16
+        ops[made]["use"] = 1.5 * use
+        add(None, None, 0.0, rd, wr, kind="a", lat=OPT["fold"] + 2.5 * use, after=[made], sem=(sem, len(topo.engines(aide[core], core))))
+        folds.append((made, sem, n, land, out, many))
+
+    fill(T.ani[:], 0, ["ani", "thi", "fill"], 72)
     dma("Y", T.lsi[:], T.ls[:], (), ["lsi"], 2000)
     dma("S", T.zin[:], T.z[:], (), ["zin"], 2000)
-    dma("Y", T.ani[0:128:16, 0:64], T.an[:], (), ["ani"], 2000)
+    a = dma("Y", T.ani[0:128:16, 0:64], T.an[:], (), ["ani"], 2000)
     dma("S", T.ani[0:128:16, 64:65], T.th[:], (), ["thi"], 2000)
-    dma("Y", T.X0[:], T.x[:], (), ["X"], 4500)
+    dma("Y", T.X0[:, 0:W], T.x[:], ["fill"], ["X"], 2200, size=524288)
 
     iota(T.jp[:, 0:17], [[-1, 17]], 16, 1, ["jp"], 17, False)
     iota(T.jc[:], [[1, 144]], 0, 0, ["jc"], 144)
     iota(T.jg[:], [[16, 8], [0, 16]], 0, 0, ["jg"], 128)
-    iota(T.jl[:], [[0, 16], [16, 2]], 0, 0, ["jl"], 32)
     fill(T.one[:], 1.0, ["one"], 256)
     fill(T.cols[:, 6:7], -32.0, ["c6"], 1)
     ts(T.pq[:, 0:17], T.jp[:, 0:17], 15, None, OP.bitwise_and, None, ["jp"], ["pq"])
@@ -189,32 +320,42 @@ def rank_program(g, core, T, topo):
             act(row[i], T.BO[:], AF.Identity, ["BO", "c16"], ["Rm%d" % i], 128, scale=T.cols[:, 16 + i:17 + i])
         else:
             ts(row[i], T.BO[:], T.cols[:, 16 + i:17 + i], None, OP.mult, None, ["BO", "c16"], ["Rm%d" % i])
-    ts(T.sl[:], T.jl[:], q, None, OP.add, None, ["jl", "i16a"], ["sl"])
     ts(T.anh[:, 0:65], T.ani[:, 0:65], -1024.0, None, OP.add, None, ["ani", "thi"], ["anh"])
     mm(T.pM[:, 0:65], row[0], T.anh[:, 0:65], "pM", "an", ["Rm0", "anh"], 65, (True, True))
-    ts(T.K[:], T.pM[:, 0:64], 32.0, 33792.0, OP.mult, OP.add, [], ["K0", "K1"], 64, bank=["pM"])
+    ts(T.K[:], T.pM[:, 0:64], 32.0, -31744.0, OP.mult, OP.add, [], ["K0", "K1"], 64, bank=["pM"])
     cp(T.L16[:], T.lsi[:], ["lsi"], ["L0", "L1"])
     at(0)
+    add("G", lambda: g.affine_select(T.Sel[:], T.one[:], [[0, 64], [-16, 8]], OP.is_equal, 0.0, 0, 1), 170 + 1024 * CYC, ["one"], ["Sel"])
+    ts(T.Tm[:, 0:1], T.pM[:, 64:65], -1.0, 776.5, OP.mult, OP.add, [], ["Tm"], bank=["pM"])
+    ts(T.TB[:], T.one[:, 0:128], T.Tm[:, 0:1], None, OP.mult, None, ["one", "Tm"], ["TB"])
     act(T.In[:], rot[0], AF.Identity, ["Pm0"], ["In"], 128, scale=-1.0)
-    ts(T.W1[:], T.jc[:], -15.0, T.cols[:, 1:2], OP.add, OP.is_equal, ["jc", "c1"], ["W1"])
-    act(T.W2[:], T.W1[:], AF.Identity, ["W1"], ["W2"], 144, scale=2.0)
-    act(T.Wn[:], T.W1[:], AF.Identity, ["W1"], ["Wn"], 144, scale=-1.0)
+    for j, v in enumerate((1.0, 2.0, -1.0)):
+        act(T.W8[:, 8 * j:8 * j + 8], T.BO[:, 0:128:16], AF.Identity, ["BO"], ["W8%d" % j], 8, scale=v)
     at(OPT["late"])
+    for j, v in ((5, -0.25), (11, 0.5), (8, 1800.0)):
+        fill(T.cols[:, j:j + 1], v, ["c%d" % j], 1)
+    ts(T.pq[:, 17:18], T.jp[:, 16:17], 7, None, OP.bitwise_and, None, ["jp"], ["p7"])
+    ts(T.pq[:, 18:19], T.jp[:, 16:17], 32, None, OP.bitwise_and, None, ["jp"], ["p32"])
+    ts(T.cols[:, 9:10], T.pq[:, 17:18], 16.0, 7.0, OP.mult, OP.add, ["p7"], ["c9"])
+    ts(T.cols[:, 10:11], T.pq[:, 18:19], 0.25, T.cols[:, 9:10], OP.mult, OP.add, ["p32", "c9"], ["c10"])
+    fill(T.Wc[:], 0.0, ["Wc0", "Wc1"], 144)
+    for m in range(2):
+        p = slice(64 * m, 64 * m + 64)
+        ts(T.Wc[p, 144 * m:144 * m + 144], T.jc[p, :], T.cols[p, 10:11], 512.0, OP.is_equal, OP.mult, ["jc", "c10"], ["Wc%d" % m])
     iota(T.jk[:], [[16, 2], [32, 16]], 8192, 0, ["jk"], 32)
     iota(T.jm[:], [[0, 4], [1, 16]], 0, 0, ["jm"], 64)
     iota(T.jb[:], [[512, 4]], 0, 0, ["jb"], 4)
     iota(T.ja[:], [[2, 2]], 0, 0, ["ja"], 2)
     iota(T.jh[:], [[1, 16], [0, 32]], 0, 0, ["jh"], 512)
     add("G", lambda: g.affine_select(T.seg[:], T.one[:], [[0, 32], [1, 16]], OP.not_equal, 0.0, 0, 0), 170 + 1024 * CYC, ["one"], ["seg"])
-    ts(T.Tm[:, 0:1], T.pM[:, 64:65], 1023.5, None, OP.add, None, [], ["Tm"], bank=["pM"])
     ts(T.Lp[:], T.lsi[:], 32.0, None, OP.add, None, ["lsi"], ["Lp0", "Lp1"])
     act(T.cols[:, 3:4], q, AF.Identity, ["i16a"], ["c3"], 1, scale=2.0, bias=1.0)
     act(T.cols[:, 4:5], q, AF.Identity, ["i16a"], ["c4"], 1, scale=32.0)
     act(T.base[:], T.jb[:], AF.Identity, ["jb", "c4"], ["base"], 4, bias=T.cols[:, 4:5])
-    act(T.W5[:], T.W1[:], AF.Identity, ["W1"], ["W5"], 144, scale=512.0)
     act(T.Wt[:], T.BO[:], AF.Identity, ["BO", "c3"], ["Wt"], 128, scale=T.cols[:, 3:4])
     act(T.ktab[:], T.jk[:], AF.Identity, ["jk", "i16a"], ["ktab"], 32, bias=q)
-    ts(T.hot[:], T.jh[:], q, 4096.0, OP.not_equal, OP.mult, ["jh", "i16a"], ["hot"], 256)
+    act(T.cols[:, 12:13], q, AF.Identity, ["i16a"], ["c12"], 1, scale=-4096.0)
+    act(T.hot[:], T.jh[:], AF.Abs, ["jh", "c12"], ["hot"], 512, scale=4096.0, bias=T.cols[:, 12:13])
     ts(T.rst[:], T.seg[:, 0:64], -65536.0, 65536.0, OP.mult, OP.add, ["seg"], ["rst"])
     ts(T.gt[:], T.jm[:], q, None, OP.is_gt, None, ["jm", "i16a"], ["gt"])
     ts(T.pick[:], T.gt[:], 4325376.0, -4194304.0, OP.mult, OP.add, ["gt"], ["pick"])
@@ -225,9 +366,6 @@ def rank_program(g, core, T, topo):
     for k in (2, 4):
         dma("Y", T.SB[:, 40 * k:40 * k + 80, :], T.SB[:, 0:80, :], names(0) + names(1), names(k) + names(k + 1), 2000)
     at(None)
-
-    def wide(Wm, i):
-        return Wm[:, 15 - i:143 - i]
 
     def lanes(buf, k, f):
         o = 40 * k + (8 if f >= 3 else 0)
@@ -240,98 +378,156 @@ def rank_program(g, core, T, topo):
         tt(T.tb[:, c:c + 32], lanes(T.RB, k, 0), lanes(T.RB, k, 3), OP.min, ["RB%d" % k], ["tb%d" % s])
         tt(out, T.tb[:, c:c + 32], lanes(T.RB, k, 4), OP.max, ["RB%d" % k, "tb%d" % s], wr)
 
-    def anchors(rnd, s, out, wr):
-        k = 2 * rnd + s
-        if s == 0:
-            tt(out, T.RA[:, 8 * rnd:8 * rnd + 4].indirect(T.al[:]), lanes(T.RB, k, 2), OP.add, ["RB%d" % k, "al", "RA%d" % rnd], wr, gat=True)
-        else:
-            cp(out, lanes(T.RB, k, 2), ["RB%d" % k], wr)
+    def anchors(rnd, out, wr):
+        tt(out, T.RA[:, 8 * rnd:8 * rnd + 4].indirect(T.al[:]), lanes(T.RB, 2 * rnd, 2), OP.add, ["RB%d" % (2 * rnd), "al", "RA%d" % rnd], wr,
+           gat=True)
 
     stg = [0]
-    xrd, Xr = ["X"], T.X0[:]
+    xrd, Xr = ["X"], T.X0[:, 0:W]
+    pD, cut4 = (T.pD0, T.pD1), OPT["cut4"]
     for rnd in range(RO):
-        Tb, tbn = (T.Tm[:, 0:1], "Tm") if rnd == 0 else (T.Tb[:, rnd:rnd + 1], "Tb%d" % rnd)
         for s in range(2):
             h, k, e = HALF[s], 2 * rnd + s, 512 * s
             so = 40 * k
             nm = lambda x: "%s%d" % (x, s)
-            L16, Lp, K = T.L16[:, h:h + 32], T.Lp[:, h:h + 32], T.K[:, h:h + 32]
+            L16, Lp, K, kn = T.L16[:, h:h + 32], T.Lp[:, h:h + 32], T.K[:, h:h + 32], nm("K")
             La, Zs, Ei = T.La[:, e:e + 512], T.Zs[:, 2 * e:2 * e + 512], T.Ei[:, e:e + 512]
+            quads = lambda x, lo=0, n=16: ["%s%d.%d" % (x, s, y) for y in range(lo, lo + n, 4)]
+            offs = lambda lo, n, js=range(4): ["%s.%d" % (x, j) for x in quads("O", lo, n) for j in js]
             at(16 * (k - 1) + OPT["names"] if s else None)
             if rnd == 0:
                 zsrc, zn = T.zin[:, h:h + 32], "zin"
             else:
                 assemble(k - 2, s, L16, [nm("L")])
                 ts(Lp, L16, 32.0, None, OP.add, None, [nm("L")], [nm("Lp")])
-                anchors(rnd - 1, s, K, [nm("K")])
                 zsrc, zn = lanes(T.RB, k - 2, 1), "RB%d" % (k - 2)
-            i0, prn = 0, []
-            for n in (OPT["start"] if k == 0 else (16,)):
+                if s == 0:
+                    anchors(rnd - 1, K, [kn])
+                else:
+                    K, kn = lanes(T.RB, k - 2, 2), zn
+            i0 = 0
+            for n in (OPT["start"] if k == 0 else (16,) if s else OPT["early"]):
                 c, w = 32 * i0, 32 * n
-                parts = range(i0, i0 + n, 4)
                 for i in range(i0, i0 + n):
                     mm(T.pLa[:, 32 * i:32 * i + 32], rot[i], L16, "pLa", ("la", k, i0), ["Pm%d" % i, nm("L")], 32, (True, True))
-                act(T.La[:, e + c:e + c + w], T.pLa[:, c:c + w], AF.Identity, ["c6"], ["La%d.%d" % (s, x) for x in parts], w, bank=["pLa"],
-                    bias=T.cols[:, 6:7])
+                act(T.La[:, e + c:e + c + w], T.pLa[:, c:c + w], AF.Identity, ["c6"], quads("La", i0, n), w, bank=["pLa"], bias=T.cols[:, 6:7])
                 mm(T.pLi[:, c:c + w], T.one[0:32, 0:128], T.one[0:32, 0:w], "pLi", ("l0", k, i0), ["one"], w, (True, False))
                 for i in range(i0, i0 + n):
                     mm(T.pLi[:, 32 * i:32 * i + 32], row[i], L16, "pLi", ("li", k, i0), ["Rm%d" % i, nm("L")], 32, "rest")
-                tt(T.pr[:, e + c:e + c + w], T.La[:, e + c:e + c + w], T.pLi[:, c:c + w], OP.mult, ["La%d.%d" % (s, x) for x in parts],
-                   ["pr%d.%d" % (s, x) for x in parts], w, bank=["pLi"])
+                tt(T.pr[:, e + c:e + c + w], T.La[:, e + c:e + c + w], T.pLi[:, c:c + w], OP.mult, quads("La", i0, n), quads("pr", i0, n), w,
+                   bank=["pLi"])
                 i0 += n
-            for i in range(16):
-                mm(T.pZ[:, i:512:16], rot[i], zsrc, "pZ", ("z", k), ["Pm%d" % i, zn], 32, (True, True))
-            act(Zs, T.pZ[:], AF.Abs, [], [nm("Zs")], 512, bank=["pZ"])
-            if "GG" in KINDS[k] or "HH" in KINDS[k]:
-                dma("Y", T.Zs[:, 2 * e + 512:2 * e + 1024], Zs, [nm("Zs")], [nm("Zt")], 2500)
-            piece, i0, eis = [], 0, []
-            for n in (OPT["pieces"] if s == 0 else (16,)):
+
+            def turned():
+                for i in range(16):
+                    mm(T.pZ[:, i:512:16], rot[i], zsrc, "pZ", ("z", k), ["Pm%d" % i, zn], 32, (True, True))
+                if rnd == 0:
+                    act(Zs, T.pZ[:], AF.Copy, [], [nm("Zs")], 512, bank=["pZ"])
+                else:
+                    act(Zs, T.pZ[:], AF.Abs, ["c11"], [nm("Zs")], 512, bank=["pZ"], scale=2.0, bias=T.cols[:, 11:12])
+                if any(nj > 1 and KINDS[k][i] != "D" for i, nj in runs(KINDS[k])):
+                    dma("Y", T.Zs[:, 2 * e + 512:2 * e + 1024], Zs, [nm("Zs")], [nm("Zt")], 1800, size=131072)
+
+            turned()
+            pK, pkn = (T.pS0, "pS0") if k == 0 else (T.pZ, "pZ")
+            late = s == 0 and rnd > 0
+            K0, k0n = (lanes(T.RB, k - 2, 2), zn) if late else (K, kn)
+            i0 = 0
+            for n in (OPT["pieces"] if k == 0 else (16,) if s else OPT["early"]):
                 c, w = e + 32 * i0, 32 * n
-                tt(T.Ni[:, c:c + w], K.indirect(T.sl[:, 0:2 * n]), T.pr[:, c:c + w], OP.add,
-                   [nm("K"), "sl"] + ["pr%d.%d" % (s, x) for x in range(i0, i0 + n, 4)], ["Ni%d" % c], w, gat=True)
-                ts(T.Ei[:, c:c + w], T.Ni[:, c:c + w], 5, 2047, OP.arith_shift_right, OP.bitwise_and, ["Ni%d" % c], ["Ei%d" % c], w)
-                cp(T.O[:, c:c + w], T.Ei[:, c:c + w], ["Ei%d" % c], ["O%d" % c], w)
-                piece += ["O%d" % c] * n; eis.append("Ei%d" % c); i0 += n
-            pD, dn = (T.pD0, T.pD1)[s], nm("pD")
+                for i in range(i0, i0 + n):
+                    mm(pK[:, 32 * i:32 * i + 32], rot[0], K0, pkn, ("k", k, i0), ["Pm0", k0n], 32, (True, True))
+                tt(T.Ni[:, c:c + w], T.pr[:, c:c + w], pK[:, c - e:c - e + w], OP.add, quads("pr", i0, n), quads("Ni", i0, n), w, bank=[pkn])
+                if late:
+                    ts(T.Nm[:, i0:i0 + n, :], T.Ni[:, c:c + w], 65504, None, OP.bitwise_and, None, quads("Ni", i0, n), quads("Nm", i0, n), w)
+                else:
+                    ts(T.Ei[:, c:c + w], T.Ni[:, c:c + w], 5, 2047, OP.arith_shift_right, OP.bitwise_and, quads("Ni", i0, n), quads("Ei", i0, n), w)
+                    cp(T.O[:, c:c + w], T.Ei[:, c:c + w], quads("Ei", i0, n), offs(i0, n), w)
+                i0 += n
+            i0 = 0
+            for n in (OPT["last"] if late else ()):
+                for j in range(4):
+                    ts(T.Oa[:, i0:i0 + n, 8 * j:8 * j + 8], T.Nm[:, i0:i0 + n, 8 * j:8 * j + 8], T.RA[:, 8 * rnd - 8 + j:8 * rnd - 7 + j], 1.0 / 32,
+                       OP.add, OP.mult, quads("Nm", i0, n) + ["RA%d" % (rnd - 1)], offs(i0, n, [j]), 8 * n)
+                i0 += n
+            Xg, xg = (T.X0[:], ["X", "Xe"]) if late else (Xr, xrd)
+            names_of = lambda i, n: T.Oa[:, i, :] if late else T.O[:, e + 32 * i:e + 32 * (i + n)]
+            for b, (lo, hi) in enumerate(((0, cut4), (cut4, 4))):
+                at(16 * k + 4 * lo)
+                mm(pD[b][:, 128 * lo:128 * hi], T.TB[:], T.Sel[:, 128 * lo:128 * hi], "pD%d" % b, ("t", k), ["Sel", "TB"], 128 * (hi - lo),
+                   (True, False))
+
+            def total(i, buf, c, j, rd):
+                b = int(i >= 4 * cut4)
+                for x in range(4):
+                    o = 128 * (i // 4) + 32 * x + 8 * (i % 4)
+                    mm(pD[b][:, o:o + 8], buf[:, c + 128 * x:c + 128 * x + 128], T.W8[:, 8 * j:8 * j + 8], "pD%d" % b, ("d", k),
+                       ["W8%d" % j] + rd, 8, "rest")
+
             for i, nj in runs(KINDS[k]):
                 at(16 * k + i)
                 kind, c0, c1 = KINDS[k][i], 8192 * s + 512 * i, 8192 * s + 512 * (i + nj)
                 dN = ["d%d" % (c0 + 512 * j) for j in range(nj)]
                 rN = ["r%d" % (c0 + 512 * j) for j in range(nj)]
-                got = Xr.indirect(T.O[:, e + 32 * i:e + 32 * (i + nj)])
+                piece = offs(i - i % 4, 4)
+                if kind in "DFGH":
+                    step = 1 if late else min(nj, OPT["sg"] // 512)
+                    for j in range(0, nj, step):
+                        act(T.d[:, c0 + 512 * j:c0 + 512 * (j + step)], Xg.indirect(names_of(i + j, step)), AF.Identity,
+                            xg + piece, dN[j:j + step], 512 * step, gat=True, scale=1.0 if kind in "DF" else -1.0)
+                if kind == "F":
+                    fold(T.d[:, c0:c1], T.Zs[:, 2 * e:2 * e + 512 * nj], T.r[:, c0:c1], 512 * nj, dN + [nm("Zs")] + [nm("Zt")] * (nj > 1), rN)
+                    for j in range(nj):
+                        c = c0 + 512 * j
+                        total(i + j, T.Zs, 2 * e, 2, [nm("Zs")])
+                        total(i + j, T.d, c, 2, [dN[j]])
+                        total(i + j, T.r, c, 1, [rN[j]])
+                    continue
                 if kind == "D":
-                    act(T.d[:, c0:c1], got, AF.Copy, xrd + [piece[i]], dN, 512 * nj, gat=True)
                     for j in range(nj):
                         c = c0 + 512 * j
                         pS, sn = (T.pS0, T.pS1)[stg[0] % 2], "pS%d" % (stg[0] % 2)
                         mm(pS[:], T.In[:], Zs, sn, ("s", stg[0]), ["In", nm("Zs")], 512)
                         mm(pS[:], rot[0], T.d[:, c:c + 512], sn, ("s", stg[0]), ["Pm0", dN[j]], 512)
                         act(T.r[:, c:c + 512], pS[:], AF.Abs, [], [rN[j]], 512, bank=[sn])
-                        mm(pD[:], wide(T.W1, i + j), T.r[:, c:c + 512], dn, ("d", k), ["W1", rN[j]], 512)
+                        total(i + j, T.r, c, 0, [rN[j]])
                         stg[0] += 1
                     continue
                 if kind in "GH":
-                    act(T.d[:, c0:c1], got, AF.Identity, xrd + [piece[i]], dN, 512 * nj, gat=True, scale=-1.0)
-                    dma("G", T.d[:, c0:c1], T.Zs[:, 2 * e:2 * e + 512 * nj], [nm("Zs"), nm("Zt")], dN, OPT["add"], 1000.0, accum_op=OP.add)
+                    dma("G", T.d[:, c0:c1], T.Zs[:, 2 * e:2 * e + 512 * nj], [nm("Zs")] + [nm("Zt")] * (nj > 1), dN, OPT["add"], 1000.0,
+                        size=2 * 131072 * nj, accum_op=OP.add)
                 else:
-                    for j in range(nj):
+                    step = nj if i >= OPT["va"] and not late else 1
+                    for j in range(0, nj, step):
                         c = c0 + 512 * j
-                        tt(T.d[:, c:c + 512], Xr.indirect(T.O[:, e + 32 * (i + j):e + 32 * (i + j) + 32]), Zs, OP.subtract,
-                           xrd + [piece[i], nm("Zs")], [dN[j]], 512, gat=True)
-                if kind in "AG":
-                    ts(T.r[:, c0:c1], T.d[:, c0:c1], 0.0, None, OP.max, None, dN, rN, 512 * nj, 0.5)
-                else:
-                    act(T.r[:, c0:c1], T.d[:, c0:c1], AF.Abs, dN, rN, 512 * nj)
+                        tt(T.d[:, c:c + 512 * step], Xg.indirect(names_of(i + j, step)), T.Zs[:, 2 * e:2 * e + 512 * step],
+                           OP.subtract, xg + piece + [nm("Zs")] + [nm("Zt")] * (step > 1), dN[j:j + step], 512 * step, gat=True)
+                step = min(nj, OPT["vr"] // 512)
+                for j in range(0, nj, step):
+                    a, b = c0 + 512 * j, c0 + 512 * (j + step)
+                    if kind in "AG":
+                        ts(T.r[:, a:b], T.d[:, a:b], 0.0, None, OP.max, None, dN[j:j + step], rN[j:j + step], 512 * step, 0.5)
+                    else:
+                        act(T.r[:, a:b], T.d[:, a:b], AF.Abs, dN[j:j + step], rN[j:j + step], 512 * step)
                 for j in range(nj):
                     c = c0 + 512 * j
                     if kind in "AG":
-                        mm(pD[:], wide(T.Wn, i + j), T.d[:, c:c + 512], dn, ("d", k), ["Wn", dN[j]], 512)
-                    mm(pD[:], wide(T.W2 if kind in "AG" else T.W1, i + j), T.r[:, c:c + 512], dn, ("d", k), ["W2", "W1", rN[j]], 512)
-            at(None)
-            ind = (T.ind0, T.ind1)[s]
-            act(ind[:], pD[:], AF.Sign, [tbn], [nm("ind")], 512, bank=[dn], bias=Tb, scale=-1.0)
-            for m in range(16):
-                mm(T.pM[:, 0:32], wide(T.W5, m), ind[:, :, m, :], "pM", ("c", k), ["W5", nm("ind")], 32)
+                        total(i + j, T.d, c, 2, [dN[j]])
+                    total(i + j, T.r, c, 1 if kind in "AG" else 0, [rN[j]])
+            for b, (lo, hi) in enumerate(((0, cut4), (cut4, 4))):
+                at(None if b else 16 * k + 4 * cut4 - 1)
+                act(T.ind[:, 128 * lo:128 * hi], pD[b][:, 128 * lo:128 * hi], AF.Sign, ["c8"], ["ind%d" % b], 128 * (hi - lo), bank=["pD%d" % b],
+                    bias=T.cols[:, 8:9], scale=-1.0)
+                for t in range(lo, hi):
+                    mm(T.pM[:, 256:384], T.ind[:, 128 * t:128 * t + 128], rot[0], "pM", ("c4", k), ["Pm0", "ind%d" % b], 128)
+            if OPT["c4"][s] == "V":
+                cp(T.C4[:], T.pM[:, 256:384], [], ["C4"], 128, bank=["pM"])
+            else:
+                act(T.C4[:], T.pM[:, 256:384], AF.Copy, [], ["C4"], 128, bank=["pM"])
+            for m in range(2):
+                for x in range(8):
+                    mm(T.pM[:, 16 * m:16 * m + 16], T.Wc[:, 144 * m + 7 - x:144 * m + 135 - x], T.C4[:, 16 * x:16 * x + 16], "pM", ("c", k, m),
+                       ["Wc0", "Wc1", "C4"], 16)
             tt(T.key[:, 0:32], T.ktab[:], T.pM[:, 0:32], OP.subtract, ["ktab"], ["keyt"], bank=["pM"])
             tt(T.key[:, 32:64], T.ktab[:], T.pM[:, 0:32], OP.add, ["ktab"], ["keyb"], bank=["pM"])
             scan(T.ksc[:, s, :], T.rst[:], T.key[:], OP.add, OP.min, ["rst", "keyt", "keyb"], [nm("ksc")], 64)
@@ -344,31 +540,40 @@ def rank_program(g, core, T, topo):
                 message(3 * rnd + 2, DISTS[0][:4], lambda j: Ac, lambda j: T.RA[:, 8 * rnd + j:8 * rnd + j + 1], True,
                         ["Ac%d" % rnd], ["RA%d" % rnd])
                 if rnd + 1 < RO:
-                    at(16 * k + 20)
+                    at(16 * k + 16)
                     ts(T.Ai[:, 0:1], Ac, 1.0 / 32, None, OP.mult, None, ["Ac%d" % rnd], ["Ai0"])
                     ts(T.Ai[:, 4:5], T.Ai[:, 0:1], 31, None, OP.bitwise_and, None, ["Ai0"], ["Ai1"])
-                    ts(T.Tb[:, rnd + 1:rnd + 2], T.Ai[:, 4:5], T.Tm[:, 0:1], None, OP.add, None, ["Ai1", "Tm"], ["Tb%d" % (rnd + 1)])
+                    ts(T.Tb[:, 0:1], T.Ai[:, 4:5], -1.0, T.Tm[:, 0:1], OP.mult, OP.add, ["Ai1", "Tm"], ["Tb"])
+                    ts(T.TB[:], T.one[:, 0:128], T.Tb[:, 0:1], None, OP.mult, None, ["one", "Tb"], ["TB"])
             at(None)
             cp(T.ki[:, 0:4], T.ksc[:, s, 15:64:16], [nm("ksc")], ["ki0"])
             ts(T.ki[:, 4:8], T.ki[:, 0:4], 511, None, OP.bitwise_and, None, ["ki0"], ["ki1"])
             cp(T.ok[:], T.ki[:, 4:8], ["ki1"], ["ok"])
-            tt(T.pw[:], La.indirect(T.ok[:, 0:2]), Lp, OP.mult, ["La%d.%d" % (s, x) for x in (0, 4, 8, 12)] + ["ok", nm("Lp")], ["pw"], gat=True)
-            tt(T.nw[:], T.pw[:], K, OP.add, ["pw", nm("K")], ["nw"])
+            tt(T.pw[:], La.indirect(T.ok[:, 0:2]), Lp, OP.mult, quads("La") + ["ok", nm("Lp")], ["pw"], gat=True)
+            tt(T.nw[:], T.pw[:], K, OP.add, ["pw", kn], ["nw"])
             ts(T.wi[:], T.nw[:], 5, 2047, OP.arith_shift_right, OP.bitwise_and, ["nw"], ["wi"])
             cp(T.ow[:], T.wi[:], ["wi"], ["ow"])
             cp(lanes(T.SB, k, 0), T.wi[:], ["wi"], ["SB%dw" % k])
             cp(lanes(T.SB, k, 3), T.hot[:].indirect(T.ok[:, 2:4]), ["hot", "ok"], ["SB%dq" % k], c=gc_(32, 50))
-            tt(lanes(T.SB, k, 4), Ei.indirect(T.ok[:, 0:2]), lanes(T.SB, k, 3), OP.subtract, eis + ["ok", "SB%dq" % k], ["SB%dp" % k], gat=True)
+            if late:
+                tt(T.vi[:, 0:32], T.pr[:, e:e + 512].indirect(T.ok[:, 0:2]), K, OP.add, quads("pr") + ["ok", kn], ["vi0"], gat=True)
+                ts(T.vi[:, 32:64], T.vi[:, 0:32], 5, 2047, OP.arith_shift_right, OP.bitwise_and, ["vi0"], ["vi1"])
+                tt(lanes(T.SB, k, 4), T.vi[:, 32:64], lanes(T.SB, k, 3), OP.subtract, ["vi1", "SB%dq" % k], ["SB%dp" % k])
+            else:
+                tt(lanes(T.SB, k, 4), Ei.indirect(T.ok[:, 0:2]), lanes(T.SB, k, 3), OP.subtract, quads("Ei") + ["ok", "SB%dq" % k],
+                   ["SB%dp" % k], gat=True)
+            at(16 * k + 8)
+            M, z0, Y = T.Mx[:, 15:512:16], T.zh[:, h:h + 32], T.Y[:, h:h + 32]
+            act(z0, T.Zs[:, 2 * e:2 * e + 512:16], AF.Identity, [nm("Zs"), "c5"], [nm("zh")], 32, scale=0.5, bias=T.cols[:, 5:6])
+            at(None)
             cut = OPT["split"] if s else 512
-            act(T.Gb[:, 0:cut], Xr.indirect(T.ow[:, 0:cut // 16]), AF.Copy, xrd + ["ow"], ["Gb0"], cut, gat=True)
+            act(T.Gb[:, 0:cut], Xr.indirect(T.ow[:, 0:cut // 16]), AF.Identity, xrd + ["ow"], ["Gb0"], cut, gat=True, scale=0.5)
             if cut < 512:
-                cp(T.Gb[:, cut:512], Xr.indirect(T.ow[:, cut // 16:32]), xrd + ["ow"], ["Gb1"], c=gc_(512 - cut, 50))
+                ts(T.Gb[:, cut:512], Xr.indirect(T.ow[:, cut // 16:32]), 0.5, None, OP.mult, None, xrd + ["ow"], ["Gb1"], c=gc_(512 - cut, 50))
             scan(T.Mx[:], T.seg[:], T.Gb[:], OP.mult, OP.max, ["seg", "Gb0", "Gb1"], ["Mx"], 256)
-            M, z0, Y = T.Mx[:, 15:512:16], T.Zs[:, 2 * e:2 * e + 512:16], T.Y[:, h:h + 32]
-            tt(T.sm[:], M, z0, OP.add, ["Mx", nm("Zs")], ["sm"])
-            ts(T.Yi[:], T.sm[:], 0.5, -0.25, OP.mult, OP.add, ["sm"], ["Yi"])
+            tt(T.Yi[:], M, z0, OP.add, ["Mx", nm("zh")], ["Yi"])
             cp(Y, T.Yi[:], ["Yi"], [nm("Y")])
-            tt(lanes(T.SB, k, 1), z0, M, OP.subtract, ["Mx", nm("Zs")], ["SB%dz" % k])
+            tt(lanes(T.SB, k, 1), z0, M, OP.subtract, ["Mx", nm("zh")], ["SB%dz" % k])
             mm(T.pM[:, 128 + h:160 + h], T.Wt[:], Y, "pM", ("u", k), ["Wt", nm("Y")], 32, (True, True))
             if s == 1:
                 pri[0] = NOW + (OPT["write"] if rnd + 1 < RO else -2e4)
@@ -378,6 +583,8 @@ def rank_program(g, core, T, topo):
                 tt(T.u31[:, 8:12], T.u31[:, 4:8], T.base[:], OP.add, ["u31", "base"], ["u32"])
                 cp(T.pl[:], T.u31[:, 8:12], ["u32"], ["pl"])
                 cp(Xr.indirect(T.pl[:]), T.Y[:], ["pl", "Y0", "Y1"], ["X"], c=50 + 64 * 4 * CYC)
+                if rnd + 1 < RO:
+                    cp(T.X0[:, W:W + 64], T.X0[:, 0:64], ["X"], ["Xe"])
                 at(None)
             cp(T.ui[:], T.pM[:, 128 + h:160 + h], [], ["ui"], bank=["pM"])
             ts(T.um[:], T.ui[:], 2047, None, OP.bitwise_and, None, ["ui"], ["um"])
@@ -397,11 +604,10 @@ def rank_program(g, core, T, topo):
         h, k = HALF[s], 2 * (RO - 1) + s
         at(None if s else 200)
         assemble(k, s, T.oL[:, h:h + 32], ["oL%d" % s])
-        dz = lanes(T.RB, k, 1)
-        ts(T.on[:, h:h + 32], dz, -1.0, None, OP.mult, None, ["RB%d" % k], ["on%d" % s])
-        tt(T.oz[:, h:h + 32], T.on[:, h:h + 32], dz, OP.max, ["RB%d" % k, "on%d" % s], ["oz%d" % s])
+        mm(T.pZ[:, 0:32], rot[0], lanes(T.RB, k, 1), "pZ", ("f", s), ["Pm0", "RB%d" % k], 32, (True, True))
+        act(T.oz[:, h:h + 32], T.pZ[:, 0:32], AF.Abs, ["c11"], ["oz%d" % s], 32, bank=["pZ"], scale=2.0, bias=T.cols[:, 11:12])
         if s == 0:
-            anchors(RO - 1, s, T.Kc[:], ["Kc"])
+            anchors(RO - 1, T.Kc[:], ["Kc"])
             ts(T.oi[:, h:h + 32], T.Kc[:], -1024.0, None, OP.add, None, ["Kc"], ["oi0"])
         else:
             ts(T.oi[:, h:h + 32], lanes(T.RB, k, 2), -1024.0, None, OP.add, None, ["RB%d" % k], ["oi1"])
@@ -411,46 +617,24 @@ def rank_program(g, core, T, topo):
     dma("S", T.yz[:], T.oz[:], ["oz0", "oz1"], (), 2000)
     dma("Y", T.ya[:], T.oa[0:128:16, :], ["oa0", "oa1"], (), 2000)
 
-    n = len(ops)
-    users = [[] for _ in range(n)]
+    users = [[] for _ in ops]
     for o in ops:
         for x in o["dep"]:
             users[x].append(o["n"])
-    way = [0.0] * n
-    for o in reversed(ops):
-        way[o["n"]] = o["cost"] + o["lat"] + max([way[u] + LAT for u in users[o["n"]]] + [0.0])
-    for o in ops:
-        way[o["n"]] += o["pri"]
-    left = [len(o["dep"]) for o in ops]
-    ready, done = [0.0] * n, [0.0] * n
-    free = {e: 0.0 for e in queue}
-    cand = [o["n"] for o in ops if not o["dep"]]
-    plan = repr((n, KINDS, OPT))
-    order = ORDER.get(plan, [])
-    if order:
-        cand = []
-    ORDER[plan] = order
-    while cand:
-        est = {x: max(ready[x], free.get(ops[x]["eng"], 0.0)) for x in cand}
-        x0 = min(cand, key=lambda x: (est[x], -way[x], x))
-        e = ops[x0]["eng"]
-        mine = [y for y in cand if ops[y]["eng"] == e]
-        x = max((y for y in mine if est[y] <= est[x0] + OPT["look"]), key=lambda y: (way[y], -y))
-        if est[x] > est[x0] + OPT["gap"]:
-            short = [y for y in mine if est[y] <= est[x0] + 1 and ops[y]["cost"] <= 115]
-            if short:
-                x = max(short, key=lambda y: (way[y], -y))
-        cand.remove(x); order.append(x)
-        if e is not None:
-            free[e] = est[x] + ops[x]["cost"]
-        done[x] = est[x] + ops[x]["cost"] + ops[x]["lat"]
-        for u in users[x]:
-            ready[u] = max(ready[u], done[x] + (0.0 if e == "P" and ops[u]["eng"] == "P" else LAT))
-            left[u] -= 1
-            if left[u] == 0:
-                cand.append(u)
+    plan = repr((len(ops), KINDS, OPT))
+    if plan not in ORDER:
+        end, ORDER[plan] = min(tighten(ops, users, first_order(ops, users, *how)) for how in OPT["tries"])
+        PLAN[0] = end
+    order = ORDER[plan]
 
     pos = {x: j for j, x in enumerate(order)}
+    if me != core:
+        rid, pnc = topo.addr(core, me)
+        for made, sem, n, land, out, many in sorted(folds, key=lambda f: pos[f[0]]):
+            g.wait_ge(T.sem[sem], many)
+            g.remote_dma(out, land, T.sem[sem], T.sem.sent, pnc, rid, topo.mask(me, core))
+        g.wait_ge(T.sem.sent, len(folds) * len(topo.engines(me, core)))
+        return
     seen, waits, marked = {}, {}, set()
     for x in order:
         o = ops[x]
@@ -472,7 +656,7 @@ def rank_program(g, core, T, topo):
     count, val = {}, {}
     size, met = {}, {}
     for o in ops:
-        size[o["grp"]] = size.get(o["grp"], 0) + 1
+        size[o["grp"]] = size.get(o["grp"], 0) + len(o.get("mm", ()))
     tail = []
     for x in order:
         o = ops[x]
@@ -483,14 +667,14 @@ def rank_program(g, core, T, topo):
             s, v = ops[y]["sem"] or (ops[y]["eng"], val[y])
             qu.wait_ge(T.sem[s], v)
         if "mm" in o:
-            out, lhsT, rhs, flags = o["mm"]
-            met[o["grp"]] = met.get(o["grp"], 0) + 1
-            last = met[o["grp"]] == size[o["grp"]]
-            if flags is None:
-                flags = (met[o["grp"]] == 1, last)
-            elif flags == "rest":
-                flags = (False, last)
-            ins = P.matmul(out, lhsT, rhs, flags[0], flags[1])
+            for out, lhsT, rhs, flags in o["mm"]:
+                met[o["grp"]] = met.get(o["grp"], 0) + 1
+                last = met[o["grp"]] == size[o["grp"]]
+                if flags is None:
+                    flags = (met[o["grp"]] == 1, last)
+                elif flags == "rest":
+                    flags = (False, last)
+                ins = P.matmul(out, lhsT, rhs, flags[0], flags[1])
         else:
             ins = o["fn"]()
         if o["kind"] == "d":

from concourse.bass import DstId, RemoteDMATransfer
from concourse.mybir import AluOpType as OP, AxisListType, ActivationFunctionType as AF

NR, RO, W = 8, 3, 2048
HALF = (32, 0)
DISTS = ((5, 6, 7, 1, 2), (1, 2, 3, 4, 5))
KINDS = ["GGAAFFAAGAAADDGA", "FFFFFFAAGGDAGGDD"] + ["FFAAFFFFAAGGAADA", "FFFFFFGGAAGAGAAD"] * 2
OPT = {"names": 0, "late": 10, "look": 90.0, "rmv": 4, "split": 256, "pieces": (4, 4, 8), "gap": 10.0, "start": (4, 4, 8), "write": 3000.0,
       "add": 2000.0, "msg": (5500.0, 5000.0, 4300.0), "sg": 1024, "vr": 512, "cut4": 3, "last": (8, 8), "c4": "VS",
       "passes": 3, "fold": 5200.0, "va": 16, "tries": [(a, b, c) for a in (0.0, 90.0, 200.0) for b in (0.0, 200.0) for c in (40.0, 120.0)], "shake": 600.0, "early": (8, 8), "lead": 1000.0,
       "row": 30.0, "rate": 25.0, "vv": 90.0}
ORDER, PLAN = {}, [0.0]

F, B, H, I, U = "float32", "bfloat16", "float16", "int32", "uint16"
SCRATCH = {
    "X0": ("sbuf", [128, W + 64], B), "Nm": ("sbuf", [128, 16, 32], I), "vi": ("sbuf", [128, 64], I), "jb": ("sbuf", [128, 4], F), "base": ("sbuf", [128, 4], F),
    "lsi": ("sbuf", [128, 64], I), "zin": ("sbuf", [128, 64], B), "ani": ("sbuf", [128, 72], I), "anh": ("sbuf", [128, 72], H),
    "jc": ("sbuf", [128, 144], B), "jg": ("sbuf", [128, 128], B), "jm": ("sbuf", [128, 64], F), "ja": ("sbuf", [128, 2], F),
    "jh": ("sbuf", [128, 512], B), "jk": ("sbuf", [128, 32], F), "jp": ("sbuf", [128, 20], I),
    "pq": ("sbuf", [128, 20], I), "cols": ("sbuf", [128, 32], F), "i16": ("sbuf", [128, 16], F),
    "Pm": ("sbuf", [128, 2048], B), "Rm": ("sbuf", [128, 2048], B),
    "BO": ("sbuf", [128, 128], B), "Wt": ("sbuf", [128, 128], B), "In": ("sbuf", [128, 128], B),
    "W8": ("sbuf", [128, 24], B), "Wc": ("sbuf", [128, 288], B), "Sel": ("sbuf", [128, 512], B), "TB": ("sbuf", [128, 128], H),
    "ind": ("sbuf", [128, 512], B), "C4": ("sbuf", [128, 128], B),
    "one": ("sbuf", [128, 512], B), "seg": ("sbuf", [128, 512], B), "rst": ("sbuf", [128, 64], F),
    "gt": ("sbuf", [128, 64], F), "pick": ("sbuf", [128, 64], F), "al": ("sbuf", [128, 2], U),
    "hot": ("sbuf", [128, 512], B), "ktab": ("sbuf", [128, 32], F),
    "SB": ("sbuf", [128, 240, 5], H), "RB": ("sbuf", [128, 240, 5], H), "RA": ("sbuf", [128, 24], F),
    "Tm": ("sbuf", [128, 4], F), "Tb": ("sbuf", [128, 4], F), "Ac": ("sbuf", [128, 12], F),
    "Ai": ("sbuf", [128, 8], I),
    "L16": ("sbuf", [128, 64], H), "Lp": ("sbuf", [128, 64], F), "K": ("sbuf", [128, 64], H), "Kc": ("sbuf", [128, 32], F),
    "ta": ("sbuf", [128, 64], F), "tb": ("sbuf", [128, 64], F),
    "La": ("sbuf", [128, 1024], F), "Zs": ("sbuf", [128, 2048], B), "pr": ("sbuf", [128, 1024], F),
    "Ni": ("sbuf", [128, 1024], I), "Ei": ("sbuf", [128, 1024], I), "O": ("sbuf", [128, 1024], U), "Oa": ("sbuf", [128, 16, 32], U),
    "d": ("sbuf", [128, 16384], B), "r": ("sbuf", [128, 16384], B),
    "key": ("sbuf", [128, 64], F), "ksc": ("sbuf", [128, 2, 64], F), "ki": ("sbuf", [128, 8], I), "ok": ("sbuf", [128, 4], U),
    "ia": ("sbuf", [128, 4], B), "pw": ("sbuf", [128, 32], F), "nw": ("sbuf", [128, 32], I), "wi": ("sbuf", [128, 32], I),
    "ow": ("sbuf", [128, 32], U), "Gb": ("sbuf", [128, 512], B), "Mx": ("sbuf", [128, 512], B),
    "zh": ("sbuf", [128, 64], F), "Yi": ("sbuf", [128, 32], I), "Y": ("sbuf", [128, 64], B), "ui": ("sbuf", [128, 32], I),
    "um": ("sbuf", [128, 32], I), "ut": ("sbuf", [128, 32], F), "up": ("sbuf", [128, 32], I), "uc": ("sbuf", [128, 32], I),
    "us": ("sbuf", [128, 64], F), "u31": ("sbuf", [128, 12], I), "pl": ("sbuf", [128, 4], U),
    "oL": ("sbuf", [128, 64], F), "oz": ("sbuf", [128, 64], B), "oi": ("sbuf", [128, 64], I),
    "oj": ("sbuf", [128, 64], I), "oa": ("sbuf", [128, 64], F),
    "pD0": ("psum", [128, 512], F), "pD1": ("psum", [128, 512], F), "pS0": ("psum", [128, 512], F), "pS1": ("psum", [128, 512], F),
    "pLa": ("psum", [128, 512], F), "pLi": ("psum", [128, 512], F), "pZ": ("psum", [128, 512], F), "pM": ("psum", [128, 512], F),
}
NDMA, NFOLD = 90, 32
SEMAPHORES = (["V", "S", "P", "G", "sent"] + ["dma%d" % k for k in range(NDMA)] + ["arr%d" % k for k in range(3 * RO)] +
              ["fold%d" % k for k in range(NFOLD)])

CYC, PEC, GAT, LAT = 1.04, 0.52, 1.56, 70.0
NOW = 1e9


def runs(kinds):
    out, i = [], 0
    while i < 16:
        n = 2 if i % 4 < 3 and kinds[i + 1] == kinds[i] else 1
        out.append((i, n)); i += n
    return out


def calls_for(src, dsts, topo, same, apart):
    near = [j for j, c in enumerate(dsts) if c in topo.cores_of(src)]
    far = [j for j in range(len(dsts)) if j not in near]
    out = topo.engines(src, dsts[far[0]])
    call = [([j], [e for e in topo.engines(src, dsts[j]) if e not in out]) for j in near]
    if same:
        return [call + [(far, out)]]
    ahead = [[([far.pop()], out)]] if apart else []
    n = len(out) // 4
    call += [([j], out[n * t:n * t + n] if t + 1 < len(far) else out[n * t:]) for t, j in enumerate(far)]
    return ahead + [call]


def first_order(ops, users, look, far, short_):
    n = len(ops)
    way = [0.0] * n
    for o in reversed(ops):
        way[o["n"]] = o["cost"] + o["lat"] + max([way[u] + LAT for u in users[o["n"]]] + [0.0])
    for o in ops:
        way[o["n"]] += o["pri"]
    left = [len(o["dep"]) for o in ops]
    ready, free, order = [0.0] * n, {}, []
    cand = [o["n"] for o in ops if not o["dep"]]
    while cand:
        est = {x: max(ready[x], free.get(ops[x]["eng"], 0.0)) for x in cand}
        x0 = min(cand, key=lambda x: (est[x], -way[x], x))
        e = ops[x0]["eng"]
        mine = [y for y in cand if ops[y]["eng"] == e]
        x = max((y for y in mine if est[y] <= est[x0] + look), key=lambda y: (way[y], -y))
        soon = [y for y in mine if ops[y]["pri"] > 0 and est[y] <= est[x0] + far]
        if soon:
            x = max(soon, key=lambda y: (way[y], -y))
        if est[x] > est[x0] + OPT["gap"]:
            short = [y for y in mine if est[y] + ops[y]["cost"] <= est[x] + short_]
            if short:
                x = max(short, key=lambda y: (way[y], -y))
        cand.remove(x); order.append(x)
        if e is not None:
            free[e] = est[x] + ops[x]["cost"]
        for u in users[x]:
            ready[u] = max(ready[u], est[x] + ops[x]["cost"] + ops[x]["lat"] + (0.0 if e == "P" and ops[u]["eng"] == "P" else LAT))
            left[u] -= 1
            if left[u] == 0:
                cand.append(u)
    return order


def place(ops, before, after, lag, rank_of, back):
    n = len(ops)
    left = [len(before[x]) for x in range(n)]
    start, busy = [0.0] * n, {}
    ready = [ops[x]["lat"] if back else 0.0 for x in range(n)]
    cand = {x for x in range(n) if not left[x]}
    end = 0.0
    while cand:
        x = min(cand, key=lambda y: (rank_of[y], y))
        cand.remove(x)
        o = ops[x]
        holds = [(o["eng"], 0.0, o["cost"])] if o["eng"] else []
        if o["use"]:
            holds.append(("Q", -o["use"] - OPT["lead"] if back else o["cost"] + OPT["lead"], o["use"]))
        t, moved = ready[x], True
        while moved:
            moved = False
            for e, off, dur in holds:
                for a, b in busy.get(e, ()):
                    if b <= t + off + 1e-3:
                        continue
                    if a >= t + off + dur - 1e-3:
                        break
                    t, moved = b - off, True
        for e, off, dur in holds:
            line = busy.setdefault(e, [])
            j = len(line)
            while j and line[j - 1][0] > t + off:
                j -= 1
            line.insert(j, (t + off, t + off + dur))
        start[x] = t
        end = max(end, t + o["cost"] + (0.0 if back else o["lat"]))
        for u in after[x]:
            ready[u] = max(ready[u], t + o["cost"] + (lag(u, x) if back else lag(x, u)))
            left[u] -= 1
            if not left[u]:
                cand.add(u)
    return start, end


def tighten(ops, users, order):
    n = len(ops)
    deps = [sorted(o["dep"]) for o in ops]
    lag = lambda a, b: ops[a]["lat"] + (0.0 if ops[a]["eng"] == "P" and ops[b]["eng"] == "P" or ops[a]["kind"] == "s" else
                                      OPT["vv"] if ops[a]["eng"] == ops[b]["eng"] == "V" else LAT)
    rank_of = [0.0] * n
    for j, x in enumerate(order):
        rank_of[x] = j
    best, seed = None, 1
    for t in range(OPT["passes"]):
        start, end = place(ops, deps, users, lag, rank_of, False)
        if best is None or end < best[0]:
            best = (end, start)
        elif t % 2:
            start = []
            for x in range(n):
                seed = (seed * 1103515245 + 12345) % 2147483648
                start.append(best[1][x] + OPT["shake"] * seed / 2147483648)
        start, end = place(ops, users, deps, lag, [-(start[x] + ops[x]["cost"]) for x in range(n)], True)
        rank_of = [-(start[x] + ops[x]["cost"]) for x in range(n)]
    return best[0], sorted(range(n), key=lambda x: (best[1][x], x))


def rank_program(g, core, T, topo):
    aide = {c: [x for x in topo.cores_of(c) if topo.die(x) == topo.die(c) and x not in T.cores][0] for c in T.cores}
    me = core
    if T.rank_of(core) is None:
        if core not in aide.values() or not any("F" in x for x in KINDS):
            return
        core = [c for c in T.cores if aide[c] == me][0]
    rank = T.rank_of(core)
    folds = []
    V, S, P = g.vector, g.scalar, g.tensor
    queue = {"V": V, "S": S, "P": P, "G": g, "Y": g.sync}
    ops, reg, ndma, sent, pri = [], {}, [0], [0], [NOW]

    def add(eng, fn, cost, rd=(), wr=(), bank=(), kind="c", lat=0.0, after=(), sem=None):
        o = {"n": len(ops), "eng": eng, "fn": fn, "cost": cost, "kind": kind, "lat": lat, "dep": set(after), "sem": sem, "grp": None,
             "pri": pri[0], "use": 0.0}
        link(o, [(x, "r") for x in rd] + [(x, None) for x in wr] + list(bank))
        ops.append(o)
        return o["n"]

    def link(o, acc):
        for x, tag in acc:
            cur, prev = reg.get(x, ((None, []), []))
            if tag is not None and cur[0] == tag:
                o["dep"].update(prev); cur[1].append(o["n"])
            else:
                o["dep"].update(cur[1]); reg[x] = ((tag, [o["n"]]), cur[1])
        o["dep"].discard(o["n"])

    def at(chunk):
        pri[0] = NOW if chunk is None else -1e6 * chunk

    def vc(n, f=1.0):
        return 20 + max(64.0, n * f) * CYC

    def gc_(n, base):
        return base + n * GAT * CYC

    def ts(out, in0, s1, s2, op0, op1, rd, wr, n=32, f=1.0, bank=(), c=None):
        if op1 is None:
            fn = lambda: V.tensor_scalar(out, in0, s1, None, op0)
        else:
            fn = lambda: V.tensor_scalar(out, in0, s1, s2, op0, op1)
        return add("V", fn, c or vc(n, f), rd, wr, [(b, "V") for b in bank])

    def tt(out, a, b, op, rd, wr, n=32, bank=(), gat=False):
        c = gc_(n, 50) if gat else vc(n, 1.0 if bank else 2.0)
        return add("V", lambda: V.tensor_tensor(out, a, b, op), c, rd, wr, [(x, "V") for x in bank])

    def cp(out, a, rd, wr, n=32, bank=(), c=None):
        return add("V", lambda: V.tensor_copy(out, a), c or vc(n), rd, wr, [(x, "V") for x in bank])

    def scan(out, a, b, op0, op1, rd, wr, n, bank=()):
        return add("V", lambda: V.tensor_tensor_scan(out, a, b, 0.0, op0, op1), vc(n), rd, wr, [(x, "V") for x in bank])

    def fill(out, v, wr, n):
        return add("V", lambda: V.memset(out, v), vc(n), (), wr)

    def act(out, a, func, rd, wr, n, bank=(), gat=False, **kw):
        return add("S", lambda: S.activation(out, a, func, **kw), gc_(n, 65) if gat else vc(n), rd, wr, [(x, "S") for x in bank])

    def mm(out, lhsT, rhs, bank, tag, rd, n, flags=None):
        o = ops[-1]
        if n <= 64 and o["grp"] == (bank, tag) and len(o["mm"]) < 4 and o["cost"] == 64 * PEC * len(o["mm"]):
            link(o, [(x, "r") for x in rd])
            o["cost"] = 64 * PEC * (len(o["mm"]) + 1)
        else:
            o = ops[add("P", None, max(64, n) * PEC, rd, (), [(bank, tag)])]
            o["mm"] = []; o["grp"] = (bank, tag)
        o["mm"].append((out, lhsT, rhs, flags))

    def dma(eng, out, a, rd, wr, lat, cost=60.0, size=0, **kw):
        s = "dma%d" % ndma[0]; ndma[0] += 1
        x = add(eng, lambda: queue[eng].dma_start(out, a, **kw), cost, rd, wr, kind="d", lat=lat, sem=(s, 16))
        if size:
            ops[x]["use"] = (128 * OPT["row"] + size / OPT["rate"]) / 16
            ops[x]["lat"] = lat + ops[x]["use"]
        return x

    def iota(out, pat, base, cm, wr, n, small=True):
        if small:
            fn = lambda: g.iota(out, pat, base, cm, allow_small_or_imprecise_dtypes=True)
        else:
            fn = lambda: g.iota(out, pat, base, cm)
        return add("G", fn, 130 + 2 * n * CYC, (), wr)

    def message(no, dists, src_of, dst_of, same, rd, wr, ahead=None):
        arr = "arr%d" % no
        dsts = [T.cores[(rank + x) % NR] for x in dists]
        made = []
        calls = calls_for(core, dsts, topo, same, ahead is not None)
        for call in calls:
            tr = []
            for js, es in call:
                ids = [topo.addr(dsts[j], core) for j in js]
                tr.append(RemoteDMATransfer(dst_ids=[DstId(rid=a, pnc=b) for a, b in ids], dma_engine_mask=sum(1 << e for e in es),
                                            remote_sem=T.sem[arr], srcs=[src_of(js[0])], dsts=[dst_of(j) for j in js]))
                sent[0] += len(es)
            made.append(add("G", lambda tr=tr: g.remote_dma_fused(tr, local_sem=T.sem.sent), 500.0,
                            rd if call is calls[-1] else ahead, (), kind="s"))
            ops[made[-1]]["use"] = OPT["row"] * (48 if same else 64 if call is calls[-1] else 16)
        total = 0
        for j, x in enumerate(dists):
            s = (rank - x) % NR
            for call in calls_for(T.cores[s], [T.cores[(s + y) % NR] for y in dists], topo, same, ahead is not None):
                total += sum(len(es) for js, es in call if j in js)
        add(None, None, 0.0, (), wr, kind="a", lat=OPT["msg"][no % 3], after=made, sem=(arr, total))

    def fold(a, b, out, n, rd, wr):
        at_ = sum(x[2] for x in folds)
        land = (T.d if at_ < 16384 else T.r)[:, at_ % 16384:at_ % 16384 + n]
        sem, mask = "fold%d" % len(folds), topo.mask(core, aide[core])
        rid, pnc = topo.addr(aide[core], core)
        tr = [RemoteDMATransfer(dst_ids=[DstId(rid=rid, pnc=pnc)], dma_engine_mask=mask, remote_sem=T.sem[sem], srcs=[a, b], dsts=[land], alu_op=2)]
        many = len(topo.engines(core, aide[core]))
        sent[0] += many
        made = add("G", lambda: g.remote_dma_fused(tr, local_sem=T.sem.sent), 600.0, rd, wr, kind="s")
        use = (128 * OPT["row"] + 256 * n / OPT["rate"]) / 16
        ops[made]["use"] = 1.5 * use
        add(None, None, 0.0, rd, wr, kind="a", lat=OPT["fold"] + 2.5 * use, after=[made], sem=(sem, len(topo.engines(aide[core], core))))
        folds.append((made, sem, n, land, out, many))

    fill(T.ani[:], 0, ["ani", "thi", "fill"], 72)
    dma("Y", T.lsi[:], T.ls[:], (), ["lsi"], 2000)
    dma("S", T.zin[:], T.z[:], (), ["zin"], 2000)
    a = dma("Y", T.ani[0:128:16, 0:64], T.an[:], (), ["ani"], 2000)
    dma("S", T.ani[0:128:16, 64:65], T.th[:], (), ["thi"], 2000)
    dma("Y", T.X0[:, 0:W], T.x[:], ["fill"], ["X"], 2200, size=524288)

    iota(T.jp[:, 0:17], [[-1, 17]], 16, 1, ["jp"], 17, False)
    iota(T.jc[:], [[1, 144]], 0, 0, ["jc"], 144)
    iota(T.jg[:], [[16, 8], [0, 16]], 0, 0, ["jg"], 128)
    fill(T.one[:], 1.0, ["one"], 256)
    fill(T.cols[:, 6:7], -32.0, ["c6"], 1)
    ts(T.pq[:, 0:17], T.jp[:, 0:17], 15, None, OP.bitwise_and, None, ["jp"], ["pq"])
    cp(T.i16[:], T.pq[:, 0:16], ["pq"], ["i16a"])
    q = T.i16[:, 0:1]
    ts(T.cols[:, 1:2], T.jp[:, 16:17], q, None, OP.subtract, None, ["jp", "i16a"], ["c1"])
    ts(T.cols[:, 16:32], T.i16[:], 0.0, None, OP.is_equal, None, ["i16a"], ["c16"])
    ts(T.BO[:], T.jg[:], T.cols[:, 1:2], None, OP.is_equal, None, ["jg", "c1"], ["BO"])
    ts(T.ta[:, 0:16], T.i16[:], T.cols[:, 1:2], None, OP.add, None, ["i16a", "c1"], ["ta0"])
    rot = [T.Pm[:, 128 * i:128 * i + 128] for i in range(16)]
    row = [T.Rm[:, 128 * i:128 * i + 128] for i in range(16)]
    for i in range(16):
        ts(rot[i], T.jc[:, 0:128], T.ta[:, i:i + 1], None, OP.is_equal, None, ["jc", "ta0"], ["Pm%d" % i])
    for i in range(16):
        if i >= OPT["rmv"]:
            act(row[i], T.BO[:], AF.Identity, ["BO", "c16"], ["Rm%d" % i], 128, scale=T.cols[:, 16 + i:17 + i])
        else:
            ts(row[i], T.BO[:], T.cols[:, 16 + i:17 + i], None, OP.mult, None, ["BO", "c16"], ["Rm%d" % i])
    ts(T.anh[:, 0:65], T.ani[:, 0:65], -1024.0, None, OP.add, None, ["ani", "thi"], ["anh"])
    mm(T.pM[:, 0:65], row[0], T.anh[:, 0:65], "pM", "an", ["Rm0", "anh"], 65, (True, True))
    ts(T.K[:], T.pM[:, 0:64], 32.0, -31744.0, OP.mult, OP.add, [], ["K0", "K1"], 64, bank=["pM"])
    cp(T.L16[:], T.lsi[:], ["lsi"], ["L0", "L1"])
    at(0)
    add("G", lambda: g.affine_select(T.Sel[:], T.one[:], [[0, 64], [-16, 8]], OP.is_equal, 0.0, 0, 1), 170 + 1024 * CYC, ["one"], ["Sel"])
    ts(T.Tm[:, 0:1], T.pM[:, 64:65], -1.0, 776.5, OP.mult, OP.add, [], ["Tm"], bank=["pM"])
    ts(T.TB[:], T.one[:, 0:128], T.Tm[:, 0:1], None, OP.mult, None, ["one", "Tm"], ["TB"])
    act(T.In[:], rot[0], AF.Identity, ["Pm0"], ["In"], 128, scale=-1.0)
    for j, v in enumerate((1.0, 2.0, -1.0)):
        act(T.W8[:, 8 * j:8 * j + 8], T.BO[:, 0:128:16], AF.Identity, ["BO"], ["W8%d" % j], 8, scale=v)
    at(OPT["late"])
    for j, v in ((5, -0.25), (11, 0.5), (8, 1800.0)):
        fill(T.cols[:, j:j + 1], v, ["c%d" % j], 1)
    ts(T.pq[:, 17:18], T.jp[:, 16:17], 7, None, OP.bitwise_and, None, ["jp"], ["p7"])
    ts(T.pq[:, 18:19], T.jp[:, 16:17], 32, None, OP.bitwise_and, None, ["jp"], ["p32"])
    ts(T.cols[:, 9:10], T.pq[:, 17:18], 16.0, 7.0, OP.mult, OP.add, ["p7"], ["c9"])
    ts(T.cols[:, 10:11], T.pq[:, 18:19], 0.25, T.cols[:, 9:10], OP.mult, OP.add, ["p32", "c9"], ["c10"])
    fill(T.Wc[:], 0.0, ["Wc0", "Wc1"], 144)
    for m in range(2):
        p = slice(64 * m, 64 * m + 64)
        ts(T.Wc[p, 144 * m:144 * m + 144], T.jc[p, :], T.cols[p, 10:11], 512.0, OP.is_equal, OP.mult, ["jc", "c10"], ["Wc%d" % m])
    iota(T.jk[:], [[16, 2], [32, 16]], 8192, 0, ["jk"], 32)
    iota(T.jm[:], [[0, 4], [1, 16]], 0, 0, ["jm"], 64)
    iota(T.jb[:], [[512, 4]], 0, 0, ["jb"], 4)
    iota(T.ja[:], [[2, 2]], 0, 0, ["ja"], 2)
    iota(T.jh[:], [[1, 16], [0, 32]], 0, 0, ["jh"], 512)
    add("G", lambda: g.affine_select(T.seg[:], T.one[:], [[0, 32], [1, 16]], OP.not_equal, 0.0, 0, 0), 170 + 1024 * CYC, ["one"], ["seg"])
    ts(T.Lp[:], T.lsi[:], 32.0, None, OP.add, None, ["lsi"], ["Lp0", "Lp1"])
    act(T.cols[:, 3:4], q, AF.Identity, ["i16a"], ["c3"], 1, scale=2.0, bias=1.0)
    act(T.cols[:, 4:5], q, AF.Identity, ["i16a"], ["c4"], 1, scale=32.0)
    act(T.base[:], T.jb[:], AF.Identity, ["jb", "c4"], ["base"], 4, bias=T.cols[:, 4:5])
    act(T.Wt[:], T.BO[:], AF.Identity, ["BO", "c3"], ["Wt"], 128, scale=T.cols[:, 3:4])
    act(T.ktab[:], T.jk[:], AF.Identity, ["jk", "i16a"], ["ktab"], 32, bias=q)
    act(T.cols[:, 12:13], q, AF.Identity, ["i16a"], ["c12"], 1, scale=-4096.0)
    act(T.hot[:], T.jh[:], AF.Abs, ["jh", "c12"], ["hot"], 512, scale=4096.0, bias=T.cols[:, 12:13])
    ts(T.rst[:], T.seg[:, 0:64], -65536.0, 65536.0, OP.mult, OP.add, ["seg"], ["rst"])
    ts(T.gt[:], T.jm[:], q, None, OP.is_gt, None, ["jm", "i16a"], ["gt"])
    ts(T.pick[:], T.gt[:], 4325376.0, -4194304.0, OP.mult, OP.add, ["gt"], ["pick"])
    ts(T.cols[:, 7:8], q, 8.0, None, OP.is_ge, None, ["i16a"], ["c7"])
    ts(T.al[:], T.ja[:], T.cols[:, 7:8], None, OP.add, None, ["ja", "c7"], ["al"])
    names = lambda k: ["SB%d%s" % (k, x) for x in "wzcpq"]
    ts(T.SB[:, 0:80, :], T.one[:, 0:400], 0.0, None, OP.mult, None, ["one"], names(0) + names(1), 200)
    for k in (2, 4):
        dma("Y", T.SB[:, 40 * k:40 * k + 80, :], T.SB[:, 0:80, :], names(0) + names(1), names(k) + names(k + 1), 2000)
    at(None)

    def lanes(buf, k, f):
        o = 40 * k + (8 if f >= 3 else 0)
        return buf[:, o:o + 32, f]

    def assemble(k, s, out, wr):
        o, c = 40 * k, 32 * s
        if s == 0:
            cp(T.RB[:, o + 24:o + 32, 3:5], T.SB[:, o + 24:o + 32, 3:5], ["SB%dp" % k, "SB%dq" % k], ["RB%d" % k])
        tt(T.tb[:, c:c + 32], lanes(T.RB, k, 0), lanes(T.RB, k, 3), OP.min, ["RB%d" % k], ["tb%d" % s])
        tt(out, T.tb[:, c:c + 32], lanes(T.RB, k, 4), OP.max, ["RB%d" % k, "tb%d" % s], wr)

    def anchors(rnd, out, wr):
        tt(out, T.RA[:, 8 * rnd:8 * rnd + 4].indirect(T.al[:]), lanes(T.RB, 2 * rnd, 2), OP.add, ["RB%d" % (2 * rnd), "al", "RA%d" % rnd], wr,
           gat=True)

    stg = [0]
    xrd, Xr = ["X"], T.X0[:, 0:W]
    pD, cut4 = (T.pD0, T.pD1), OPT["cut4"]
    for rnd in range(RO):
        for s in range(2):
            h, k, e = HALF[s], 2 * rnd + s, 512 * s
            so = 40 * k
            nm = lambda x: "%s%d" % (x, s)
            L16, Lp, K, kn = T.L16[:, h:h + 32], T.Lp[:, h:h + 32], T.K[:, h:h + 32], nm("K")
            La, Zs, Ei = T.La[:, e:e + 512], T.Zs[:, 2 * e:2 * e + 512], T.Ei[:, e:e + 512]
            quads = lambda x, lo=0, n=16: ["%s%d.%d" % (x, s, y) for y in range(lo, lo + n, 4)]
            offs = lambda lo, n, js=range(4): ["%s.%d" % (x, j) for x in quads("O", lo, n) for j in js]
            at(16 * (k - 1) + OPT["names"] if s else None)
            if rnd == 0:
                zsrc, zn = T.zin[:, h:h + 32], "zin"
            else:
                assemble(k - 2, s, L16, [nm("L")])
                ts(Lp, L16, 32.0, None, OP.add, None, [nm("L")], [nm("Lp")])
                zsrc, zn = lanes(T.RB, k - 2, 1), "RB%d" % (k - 2)
                if s == 0:
                    anchors(rnd - 1, K, [kn])
                else:
                    K, kn = lanes(T.RB, k - 2, 2), zn
            i0 = 0
            for n in (OPT["start"] if k == 0 else (16,) if s else OPT["early"]):
                c, w = 32 * i0, 32 * n
                for i in range(i0, i0 + n):
                    mm(T.pLa[:, 32 * i:32 * i + 32], rot[i], L16, "pLa", ("la", k, i0), ["Pm%d" % i, nm("L")], 32, (True, True))
                act(T.La[:, e + c:e + c + w], T.pLa[:, c:c + w], AF.Identity, ["c6"], quads("La", i0, n), w, bank=["pLa"], bias=T.cols[:, 6:7])
                mm(T.pLi[:, c:c + w], T.one[0:32, 0:128], T.one[0:32, 0:w], "pLi", ("l0", k, i0), ["one"], w, (True, False))
                for i in range(i0, i0 + n):
                    mm(T.pLi[:, 32 * i:32 * i + 32], row[i], L16, "pLi", ("li", k, i0), ["Rm%d" % i, nm("L")], 32, "rest")
                tt(T.pr[:, e + c:e + c + w], T.La[:, e + c:e + c + w], T.pLi[:, c:c + w], OP.mult, quads("La", i0, n), quads("pr", i0, n), w,
                   bank=["pLi"])
                i0 += n

            def turned():
                for i in range(16):
                    mm(T.pZ[:, i:512:16], rot[i], zsrc, "pZ", ("z", k), ["Pm%d" % i, zn], 32, (True, True))
                if rnd == 0:
                    act(Zs, T.pZ[:], AF.Copy, [], [nm("Zs")], 512, bank=["pZ"])
                else:
                    act(Zs, T.pZ[:], AF.Abs, ["c11"], [nm("Zs")], 512, bank=["pZ"], scale=2.0, bias=T.cols[:, 11:12])
                if any(nj > 1 and KINDS[k][i] != "D" for i, nj in runs(KINDS[k])):
                    dma("Y", T.Zs[:, 2 * e + 512:2 * e + 1024], Zs, [nm("Zs")], [nm("Zt")], 1800, size=131072)

            turned()
            pK, pkn = (T.pS0, "pS0") if k == 0 else (T.pZ, "pZ")
            late = s == 0 and rnd > 0
            K0, k0n = (lanes(T.RB, k - 2, 2), zn) if late else (K, kn)
            i0 = 0
            for n in (OPT["pieces"] if k == 0 else (16,) if s else OPT["early"]):
                c, w = e + 32 * i0, 32 * n
                for i in range(i0, i0 + n):
                    mm(pK[:, 32 * i:32 * i + 32], rot[0], K0, pkn, ("k", k, i0), ["Pm0", k0n], 32, (True, True))
                tt(T.Ni[:, c:c + w], T.pr[:, c:c + w], pK[:, c - e:c - e + w], OP.add, quads("pr", i0, n), quads("Ni", i0, n), w, bank=[pkn])
                if late:
                    ts(T.Nm[:, i0:i0 + n, :], T.Ni[:, c:c + w], 65504, None, OP.bitwise_and, None, quads("Ni", i0, n), quads("Nm", i0, n), w)
                else:
                    ts(T.Ei[:, c:c + w], T.Ni[:, c:c + w], 5, 2047, OP.arith_shift_right, OP.bitwise_and, quads("Ni", i0, n), quads("Ei", i0, n), w)
                    cp(T.O[:, c:c + w], T.Ei[:, c:c + w], quads("Ei", i0, n), offs(i0, n), w)
                i0 += n
            i0 = 0
            for n in (OPT["last"] if late else ()):
                for j in range(4):
                    ts(T.Oa[:, i0:i0 + n, 8 * j:8 * j + 8], T.Nm[:, i0:i0 + n, 8 * j:8 * j + 8], T.RA[:, 8 * rnd - 8 + j:8 * rnd - 7 + j], 1.0 / 32,
                       OP.add, OP.mult, quads("Nm", i0, n) + ["RA%d" % (rnd - 1)], offs(i0, n, [j]), 8 * n)
                i0 += n
            Xg, xg = (T.X0[:], ["X", "Xe"]) if late else (Xr, xrd)
            names_of = lambda i, n: T.Oa[:, i, :] if late else T.O[:, e + 32 * i:e + 32 * (i + n)]
            for b, (lo, hi) in enumerate(((0, cut4), (cut4, 4))):
                at(16 * k + 4 * lo)
                mm(pD[b][:, 128 * lo:128 * hi], T.TB[:], T.Sel[:, 128 * lo:128 * hi], "pD%d" % b, ("t", k), ["Sel", "TB"], 128 * (hi - lo),
                   (True, False))

            def total(i, buf, c, j, rd):
                b = int(i >= 4 * cut4)
                for x in range(4):
                    o = 128 * (i // 4) + 32 * x + 8 * (i % 4)
                    mm(pD[b][:, o:o + 8], buf[:, c + 128 * x:c + 128 * x + 128], T.W8[:, 8 * j:8 * j + 8], "pD%d" % b, ("d", k),
                       ["W8%d" % j] + rd, 8, "rest")

            for i, nj in runs(KINDS[k]):
                at(16 * k + i)
                kind, c0, c1 = KINDS[k][i], 8192 * s + 512 * i, 8192 * s + 512 * (i + nj)
                dN = ["d%d" % (c0 + 512 * j) for j in range(nj)]
                rN = ["r%d" % (c0 + 512 * j) for j in range(nj)]
                piece = offs(i - i % 4, 4)
                if kind in "DFGH":
                    step = 1 if late else min(nj, OPT["sg"] // 512)
                    for j in range(0, nj, step):
                        act(T.d[:, c0 + 512 * j:c0 + 512 * (j + step)], Xg.indirect(names_of(i + j, step)), AF.Identity,
                            xg + piece, dN[j:j + step], 512 * step, gat=True, scale=1.0 if kind in "DF" else -1.0)
                if kind == "F":
                    fold(T.d[:, c0:c1], T.Zs[:, 2 * e:2 * e + 512 * nj], T.r[:, c0:c1], 512 * nj, dN + [nm("Zs")] + [nm("Zt")] * (nj > 1), rN)
                    for j in range(nj):
                        c = c0 + 512 * j
                        total(i + j, T.Zs, 2 * e, 2, [nm("Zs")])
                        total(i + j, T.d, c, 2, [dN[j]])
                        total(i + j, T.r, c, 1, [rN[j]])
                    continue
                if kind == "D":
                    for j in range(nj):
                        c = c0 + 512 * j
                        pS, sn = (T.pS0, T.pS1)[stg[0] % 2], "pS%d" % (stg[0] % 2)
                        mm(pS[:], T.In[:], Zs, sn, ("s", stg[0]), ["In", nm("Zs")], 512)
                        mm(pS[:], rot[0], T.d[:, c:c + 512], sn, ("s", stg[0]), ["Pm0", dN[j]], 512)
                        act(T.r[:, c:c + 512], pS[:], AF.Abs, [], [rN[j]], 512, bank=[sn])
                        total(i + j, T.r, c, 0, [rN[j]])
                        stg[0] += 1
                    continue
                if kind in "GH":
                    dma("G", T.d[:, c0:c1], T.Zs[:, 2 * e:2 * e + 512 * nj], [nm("Zs")] + [nm("Zt")] * (nj > 1), dN, OPT["add"], 1000.0,
                        size=2 * 131072 * nj, accum_op=OP.add)
                else:
                    step = nj if i >= OPT["va"] and not late else 1
                    for j in range(0, nj, step):
                        c = c0 + 512 * j
                        tt(T.d[:, c:c + 512 * step], Xg.indirect(names_of(i + j, step)), T.Zs[:, 2 * e:2 * e + 512 * step],
                           OP.subtract, xg + piece + [nm("Zs")] + [nm("Zt")] * (step > 1), dN[j:j + step], 512 * step, gat=True)
                step = min(nj, OPT["vr"] // 512)
                for j in range(0, nj, step):
                    a, b = c0 + 512 * j, c0 + 512 * (j + step)
                    if kind in "AG":
                        ts(T.r[:, a:b], T.d[:, a:b], 0.0, None, OP.max, None, dN[j:j + step], rN[j:j + step], 512 * step, 0.5)
                    else:
                        act(T.r[:, a:b], T.d[:, a:b], AF.Abs, dN[j:j + step], rN[j:j + step], 512 * step)
                for j in range(nj):
                    c = c0 + 512 * j
                    if kind in "AG":
                        total(i + j, T.d, c, 2, [dN[j]])
                    total(i + j, T.r, c, 1 if kind in "AG" else 0, [rN[j]])
            for b, (lo, hi) in enumerate(((0, cut4), (cut4, 4))):
                at(None if b else 16 * k + 4 * cut4 - 1)
                act(T.ind[:, 128 * lo:128 * hi], pD[b][:, 128 * lo:128 * hi], AF.Sign, ["c8"], ["ind%d" % b], 128 * (hi - lo), bank=["pD%d" % b],
                    bias=T.cols[:, 8:9], scale=-1.0)
                for t in range(lo, hi):
                    mm(T.pM[:, 256:384], T.ind[:, 128 * t:128 * t + 128], rot[0], "pM", ("c4", k), ["Pm0", "ind%d" % b], 128)
            if OPT["c4"][s] == "V":
                cp(T.C4[:], T.pM[:, 256:384], [], ["C4"], 128, bank=["pM"])
            else:
                act(T.C4[:], T.pM[:, 256:384], AF.Copy, [], ["C4"], 128, bank=["pM"])
            for m in range(2):
                for x in range(8):
                    mm(T.pM[:, 16 * m:16 * m + 16], T.Wc[:, 144 * m + 7 - x:144 * m + 135 - x], T.C4[:, 16 * x:16 * x + 16], "pM", ("c", k, m),
                       ["Wc0", "Wc1", "C4"], 16)
            tt(T.key[:, 0:32], T.ktab[:], T.pM[:, 0:32], OP.subtract, ["ktab"], ["keyt"], bank=["pM"])
            tt(T.key[:, 32:64], T.ktab[:], T.pM[:, 0:32], OP.add, ["ktab"], ["keyb"], bank=["pM"])
            scan(T.ksc[:, s, :], T.rst[:], T.key[:], OP.add, OP.min, ["rst", "keyt", "keyb"], [nm("ksc")], 64)
            if s == 1:
                pri[0] = 2 * NOW
                Ac = T.Ac[:, 4 * rnd:4 * rnd + 1]
                ts(T.ia[:], T.ksc[:, :, 15:32:16], 7680.0, 32.0, OP.is_lt, OP.mult, ["ksc0", "ksc1"], ["ia"])
                mm(T.pM[:, 64:68], T.BO[:], T.ia[:], "pM", ("a", k), ["BO", "ia"], 4, (True, True))
                add("V", lambda Ac=Ac: V.tensor_reduce(Ac, T.pM[:, 64:68], AxisListType.X, OP.add), vc(4), (), ["Ac%d" % rnd], [("pM", "V")])
                message(3 * rnd + 2, DISTS[0][:4], lambda j: Ac, lambda j: T.RA[:, 8 * rnd + j:8 * rnd + j + 1], True,
                        ["Ac%d" % rnd], ["RA%d" % rnd])
                if rnd + 1 < RO:
                    at(16 * k + 16)
                    ts(T.Ai[:, 0:1], Ac, 1.0 / 32, None, OP.mult, None, ["Ac%d" % rnd], ["Ai0"])
                    ts(T.Ai[:, 4:5], T.Ai[:, 0:1], 31, None, OP.bitwise_and, None, ["Ai0"], ["Ai1"])
                    ts(T.Tb[:, 0:1], T.Ai[:, 4:5], -1.0, T.Tm[:, 0:1], OP.mult, OP.add, ["Ai1", "Tm"], ["Tb"])
                    ts(T.TB[:], T.one[:, 0:128], T.Tb[:, 0:1], None, OP.mult, None, ["one", "Tb"], ["TB"])
            at(None)
            cp(T.ki[:, 0:4], T.ksc[:, s, 15:64:16], [nm("ksc")], ["ki0"])
            ts(T.ki[:, 4:8], T.ki[:, 0:4], 511, None, OP.bitwise_and, None, ["ki0"], ["ki1"])
            cp(T.ok[:], T.ki[:, 4:8], ["ki1"], ["ok"])
            tt(T.pw[:], La.indirect(T.ok[:, 0:2]), Lp, OP.mult, quads("La") + ["ok", nm("Lp")], ["pw"], gat=True)
            tt(T.nw[:], T.pw[:], K, OP.add, ["pw", kn], ["nw"])
            ts(T.wi[:], T.nw[:], 5, 2047, OP.arith_shift_right, OP.bitwise_and, ["nw"], ["wi"])
            cp(T.ow[:], T.wi[:], ["wi"], ["ow"])
            cp(lanes(T.SB, k, 0), T.wi[:], ["wi"], ["SB%dw" % k])
            cp(lanes(T.SB, k, 3), T.hot[:].indirect(T.ok[:, 2:4]), ["hot", "ok"], ["SB%dq" % k], c=gc_(32, 50))
            if late:
                tt(T.vi[:, 0:32], T.pr[:, e:e + 512].indirect(T.ok[:, 0:2]), K, OP.add, quads("pr") + ["ok", kn], ["vi0"], gat=True)
                ts(T.vi[:, 32:64], T.vi[:, 0:32], 5, 2047, OP.arith_shift_right, OP.bitwise_and, ["vi0"], ["vi1"])
                tt(lanes(T.SB, k, 4), T.vi[:, 32:64], lanes(T.SB, k, 3), OP.subtract, ["vi1", "SB%dq" % k], ["SB%dp" % k])
            else:
                tt(lanes(T.SB, k, 4), Ei.indirect(T.ok[:, 0:2]), lanes(T.SB, k, 3), OP.subtract, quads("Ei") + ["ok", "SB%dq" % k],
                   ["SB%dp" % k], gat=True)
            at(16 * k + 8)
            M, z0, Y = T.Mx[:, 15:512:16], T.zh[:, h:h + 32], T.Y[:, h:h + 32]
            act(z0, T.Zs[:, 2 * e:2 * e + 512:16], AF.Identity, [nm("Zs"), "c5"], [nm("zh")], 32, scale=0.5, bias=T.cols[:, 5:6])
            at(None)
            cut = OPT["split"] if s else 512
            act(T.Gb[:, 0:cut], Xr.indirect(T.ow[:, 0:cut // 16]), AF.Identity, xrd + ["ow"], ["Gb0"], cut, gat=True, scale=0.5)
            if cut < 512:
                ts(T.Gb[:, cut:512], Xr.indirect(T.ow[:, cut // 16:32]), 0.5, None, OP.mult, None, xrd + ["ow"], ["Gb1"], c=gc_(512 - cut, 50))
            scan(T.Mx[:], T.seg[:], T.Gb[:], OP.mult, OP.max, ["seg", "Gb0", "Gb1"], ["Mx"], 256)
            tt(T.Yi[:], M, z0, OP.add, ["Mx", nm("zh")], ["Yi"])
            cp(Y, T.Yi[:], ["Yi"], [nm("Y")])
            tt(lanes(T.SB, k, 1), z0, M, OP.subtract, ["Mx", nm("zh")], ["SB%dz" % k])
            mm(T.pM[:, 128 + h:160 + h], T.Wt[:], Y, "pM", ("u", k), ["Wt", nm("Y")], 32, (True, True))
            if s == 1:
                pri[0] = NOW + (OPT["write"] if rnd + 1 < RO else -2e4)
                scan(T.us[:], T.pick[:], T.pM[:, 128:192], OP.add, OP.max, ["pick"], ["us"], 64, bank=["pM"])
                cp(T.u31[:, 0:4], T.us[:, 15:64:16], ["us"], ["u30"])
                ts(T.u31[:, 4:8], T.u31[:, 0:4], 31, None, OP.bitwise_and, None, ["u30"], ["u31"])
                tt(T.u31[:, 8:12], T.u31[:, 4:8], T.base[:], OP.add, ["u31", "base"], ["u32"])
                cp(T.pl[:], T.u31[:, 8:12], ["u32"], ["pl"])
                cp(Xr.indirect(T.pl[:]), T.Y[:], ["pl", "Y0", "Y1"], ["X"], c=50 + 64 * 4 * CYC)
                if rnd + 1 < RO:
                    cp(T.X0[:, W:W + 64], T.X0[:, 0:64], ["X"], ["Xe"])
                at(None)
            cp(T.ui[:], T.pM[:, 128 + h:160 + h], [], ["ui"], bank=["pM"])
            ts(T.um[:], T.ui[:], 2047, None, OP.bitwise_and, None, ["ui"], ["um"])
            ts(T.ut[:], T.um[:], 1184.0, None, OP.add, None, ["um"], ["ut"])
            tt(T.up[:], T.um[:], T.ut[:], OP.mult, ["um", "ut"], ["up"])
            ts(T.uc[:], T.up[:], 65504, None, OP.bitwise_and, None, ["up"], ["uc"])
            if s == 0:
                ts(lanes(T.SB, k, 2), T.uc[:], -64512.0, None, OP.add, None, ["uc"], ["SB%dc" % k])
            else:
                ts(lanes(T.SB, k, 2), T.uc[:], -64512.0, Ac, OP.add, OP.add, ["uc", "Ac%d" % rnd], ["SB%dc" % k])
            message(3 * rnd + s, DISTS[s], lambda j: T.SB[:, so + 8 * j:so + 8 * j + 8, :], lambda j: T.RB[:, so + 8 * j:so + 8 * j + 8, :],
                    False, names(k), ["RB%d" % k], ahead=["SB%dp" % k, "SB%dq" % k] if s else None)
    dma("Y", T.yx[:, 0:W // 2], T.X0[:, 0:W // 2], xrd, (), 3500)
    dma("S", T.yx[:, W // 2:W], T.X0[:, W // 2:W], xrd, (), 3500)

    for s in range(2):
        h, k = HALF[s], 2 * (RO - 1) + s
        at(None if s else 200)
        assemble(k, s, T.oL[:, h:h + 32], ["oL%d" % s])
        mm(T.pZ[:, 0:32], rot[0], lanes(T.RB, k, 1), "pZ", ("f", s), ["Pm0", "RB%d" % k], 32, (True, True))
        act(T.oz[:, h:h + 32], T.pZ[:, 0:32], AF.Abs, ["c11"], ["oz%d" % s], 32, bank=["pZ"], scale=2.0, bias=T.cols[:, 11:12])
        if s == 0:
            anchors(RO - 1, T.Kc[:], ["Kc"])
            ts(T.oi[:, h:h + 32], T.Kc[:], -1024.0, None, OP.add, None, ["Kc"], ["oi0"])
        else:
            ts(T.oi[:, h:h + 32], lanes(T.RB, k, 2), -1024.0, None, OP.add, None, ["RB%d" % k], ["oi1"])
        ts(T.oj[:, h:h + 32], T.oi[:, h:h + 32], 5, 2047, OP.arith_shift_right, OP.bitwise_and, ["oi%d" % s], ["oj%d" % s])
        cp(T.oa[:, h:h + 32], T.oj[:, h:h + 32], ["oj%d" % s], ["oa%d" % s])
    dma("Y", T.yl[:], T.oL[:], ["oL0", "oL1"], (), 2000)
    dma("S", T.yz[:], T.oz[:], ["oz0", "oz1"], (), 2000)
    dma("Y", T.ya[:], T.oa[0:128:16, :], ["oa0", "oa1"], (), 2000)

    users = [[] for _ in ops]
    for o in ops:
        for x in o["dep"]:
            users[x].append(o["n"])
    plan = repr((len(ops), KINDS, OPT))
    if plan not in ORDER:
        end, ORDER[plan] = min(tighten(ops, users, first_order(ops, users, *how)) for how in OPT["tries"])
        PLAN[0] = end
    order = ORDER[plan]

    pos = {x: j for j, x in enumerate(order)}
    if me != core:
        rid, pnc = topo.addr(core, me)
        for made, sem, n, land, out, many in sorted(folds, key=lambda f: pos[f[0]]):
            g.wait_ge(T.sem[sem], many)
            g.remote_dma(out, land, T.sem[sem], T.sem.sent, pnc, rid, topo.mask(me, core))
        g.wait_ge(T.sem.sent, len(folds) * len(topo.engines(me, core)))
        return
    seen, waits, marked = {}, {}, set()
    for x in order:
        o = ops[x]
        if o["eng"] is None:
            continue
        need, w = {}, []
        for y in o["dep"]:
            p = ops[y]
            if p["kind"] == "s" or (p["eng"] == "P" and o["eng"] == "P"):
                continue
            key = p["sem"][0] if p["sem"] else p["eng"]
            if key not in need or pos[y] > pos[need[key]]:
                need[key] = y
        for key in sorted(need):
            y = need[key]
            if seen.get((o["eng"], key), -1) < pos[y]:
                seen[(o["eng"], key)] = pos[y]; w.append(y); marked.add(y)
        waits[x] = w
    count, val = {}, {}
    size, met = {}, {}
    for o in ops:
        size[o["grp"]] = size.get(o["grp"], 0) + len(o.get("mm", ()))
    tail = []
    for x in order:
        o = ops[x]
        if o["eng"] is None:
            continue
        qu = queue[o["eng"]]
        for y in waits[x]:
            s, v = ops[y]["sem"] or (ops[y]["eng"], val[y])
            qu.wait_ge(T.sem[s], v)
        if "mm" in o:
            for out, lhsT, rhs, flags in o["mm"]:
                met[o["grp"]] = met.get(o["grp"], 0) + 1
                last = met[o["grp"]] == size[o["grp"]]
                if flags is None:
                    flags = (met[o["grp"]] == 1, last)
                elif flags == "rest":
                    flags = (False, last)
                ins = P.matmul(out, lhsT, rhs, flags[0], flags[1])
        else:
            ins = o["fn"]()
        if o["kind"] == "d":
            ins.then_inc(T.sem[o["sem"][0]], 16)
            if x not in marked:
                tail.append((qu, o["sem"]))
        elif x in marked:
            count[o["eng"]] = count.get(o["eng"], 0) + 1
            val[x] = count[o["eng"]]
            ins.then_inc(T.sem[o["eng"]], 1)
    for qu, (s, v) in tail:
        qu.wait_ge(T.sem[s], v)
    g.wait_ge(T.sem.sent, sent[0])
